import numpy as np
import ml_dtypes


def mxq(x, axis, fmt="e4m3"):
    dtype, down = {"e4m3": (ml_dtypes.float8_e4m3fn, 7), "e5m2": (ml_dtypes.float8_e5m2, 14)}[fmt]
    v = np.moveaxis(np.asarray(x, np.float32).astype(ml_dtypes.bfloat16).astype(np.float64), axis, -1)
    blocks = v.reshape(v.shape[:-1] + (-1, 32))
    amax = np.abs(blocks).max(-1, keepdims=True)
    byte = np.maximum(np.where(amax > 0, np.frexp(amax)[1] - 1 + 127, 0) - down, 1)
    scale = np.exp2(byte - 127.0)
    codes = (blocks / scale).astype(np.float32).astype(dtype).astype(np.float64)
    return np.moveaxis((codes * scale).reshape(v.shape), -1, axis)


WIDE = False


def mx_kscale(k):
    if not WIDE:
        return np.ones(k)
    levels = np.array([10, -10, 5, -5, 0])
    if k % 512:
        return np.exp2(np.random.permutation(np.resize(levels, k // 32))).repeat(32)
    a = np.empty((k // 512, 16))
    for p in range(k // 512):
        a[p, :8] = np.random.permutation(np.resize(levels, 8))
        for g in range(8):
            far = levels[np.abs(levels - a[p, g]) >= 10]
            a[p, g + 8] = far[np.random.randint(len(far))]
    return np.exp2(a.ravel()).repeat(32)


BF16 = ml_dtypes.bfloat16


def bf(x):
    return np.asarray(x, np.float32).astype(BF16)


def f64(x):
    return np.asarray(x).astype(np.float64)

def planes(Y):
    n, m = Y.shape
    b = f64(bf(Y)).reshape(n // 32, 32, m)
    amax = np.abs(b).max(1)
    byte = np.clip(np.where(amax > 0, np.frexp(amax)[1] - 1 + 127 - 7, 1), 1, 254)
    codes = (b * np.exp2(127.0 - byte)[:, None, :]).reshape(n, m).astype(np.float32).astype(ml_dtypes.float8_e4m3fn).view(np.uint8)
    words = codes.reshape(n // 512, 128, 4, m).transpose(0, 1, 3, 2)
    return np.ascontiguousarray(words), np.ascontiguousarray(byte.astype(np.uint8).reshape(n // 512, 16, m))


T, D, F, S = 1024, 512, 2048, 768

def setup_inputs():
    s = mx_kscale(D)
    t = mx_kscale(T)
    times = np.random.rand(T)
    freqs = 16.0 * np.random.randn(D // 2)
    phase = 2.0 * np.pi * times[:, None] * freqs[None, :]
    emb = np.sqrt(2.0) * np.concatenate([np.cos(phase), np.sin(phase)], axis=1)
    w1 = np.random.randn(D, F) / np.sqrt(D)
    time_scale = np.exp(0.3 * np.random.randn(T))
    blend = 2.0 * np.random.randn(S, T) / np.sqrt(T)
    bias = 0.3 * np.random.randn(F)
    gain = np.exp(0.8 * np.random.randn(F))
    return {
        "emb": bf(emb * s[None, :]),
        "w1": bf(w1 / s[:, None]),
        "time_scale": bf(time_scale * t),
        "blend": bf(blend / t[None, :]),
        "bias": bf(bias),
        "gain": bf(gain),
    }

def reference(emb, w1, time_scale, blend, bias, gain):
    a = mxq(f64(emb), 1, "e4m3") @ mxq(f64(w1), 0, "e4m3")
    z = a / (1.0 + np.exp(-a)) * f64(time_scale)[:, None]
    c = mxq(f64(blend), 1, "e4m3") @ mxq(z, 0, "e4m3")
    c = c + f64(bias)[None, :]
    y = c / (1.0 + np.exp(-c)) * f64(gain)[None, :]
    words, scales = planes(y.T)
    return y, words, scales

@@ -1,0 +1,355 @@
+from contextlib import ExitStack
+
+import concourse.mybir as mybir
+from concourse.masks import make_identity
+
+T, D, F, S = 1024, 512, 2048, 768
+FLOPS = 2 * T * D * F + 2 * S * T * F
+
+F32 = mybir.dt.float32
+BF16 = mybir.dt.bfloat16
+I32 = mybir.dt.int32
+U32 = mybir.dt.uint32
+U8 = mybir.dt.uint8
+FP8X4 = mybir.dt.float8_e4m3fn_x4
+SILU = mybir.ActivationFunctionType.Silu
+MULT = mybir.AluOpType.mult
+
+P = 128
+PACK = 4
+K_PASS = P * PACK
+BANK = 512
+BANKS = 8
+TIME_PASSES = T // K_PASS
+GROUPS = F // K_PASS
+UNITS = GROUPS * PACK
+WIDE = 512
+NARROW = S - WIDE
+PIECE = 256
+PIECES = S // PIECE
+
+
+def tile_timestep_blend_conditioning_h3_kernel(
+    tc, emb, w1, time_scale, blend, bias, gain, out_0, out_1, out_2
+):
+    nc = tc.nc
+    with ExitStack() as ctx:
+        keep = ctx.enter_context(tc.tile_pool(name="keep", bufs=1))
+        psum = ctx.enter_context(tc.psum_pool(name="psum", bufs=1))
+        ctx.enter_context(tc.manual_schedule())
+
+        uses = {}
+
+        def ring(pool, tag, depth, shape, dtype):
+            n = uses.get(tag, 0)
+            uses[tag] = n + 1
+            return pool.tile(shape, dtype, name=tag, tag="%s%d" % (tag, n % depth), align_bytes=64)
+
+        def next_bank():
+            n = uses.get("bank", 0)
+            uses["bank"] = n + 1
+            return psum.tile([P, BANK], F32, name="bank", tag="bank%d" % (n % BANKS))
+
+        def kept(name, shape, dtype):
+            return keep.tile(shape, dtype, name=name, tag=name, align_bytes=64)
+
+        emb_rows = emb.rearrange("(h m t) k -> h m t k", m=P, t=PACK)
+        emb_raw = {}
+        w1_raw = {}
+        blend_raw = {}
+
+        def load_emb(h, pair):
+            emb_raw[h, pair] = kept("emb_raw%d_%d" % (h, pair), [P, 2, D], BF16)
+            nc.sync.dma_start(out=emb_raw[h, pair][:], in_=emb_rows[h, :, 2 * pair : 2 * pair + 2, :])
+
+        def load_w1(g):
+            w1_raw[g] = kept("w1_raw%d" % g, [P, PACK, K_PASS], BF16)
+            cols = w1[:, g * K_PASS : (g + 1) * K_PASS]
+            nc.sync.dma_start(out=w1_raw[g][:], in_=cols.rearrange("(p j) c -> p j c", j=PACK))
+
+        def load_blend(piece):
+            blend_raw[piece] = kept("blend_raw%d" % piece, [P, 2, T], BF16)
+            rows = blend[piece * PIECE : (piece + 1) * PIECE, :]
+            nc.sync.dma_start(out=blend_raw[piece][:], in_=rows.rearrange("(a m) k -> m a k", m=P))
+
+        load_emb(0, 0)
+        load_emb(0, 1)
+        load_w1(0)
+        load_emb(1, 0)
+        load_emb(1, 1)
+        scale_sb = kept("scale_sb", [P, TIME_PASSES, PACK], BF16)
+        bias_sb = kept("bias_sb", [P, GROUPS, PACK], BF16)
+        gain_sb = kept("gain_sb", [P, GROUPS, PACK], BF16)
+        nc.scalar.dma_start(out=scale_sb[:], in_=time_scale.rearrange("(h p t) -> p h t", p=P, t=PACK))
+        load_blend(0)
+        load_w1(1)
+        load_blend(1)
+        load_blend(2)
+        nc.sync.dma_start(out=bias_sb[:], in_=bias.rearrange("(g p t) -> p g t", p=P, t=PACK))
+        nc.sync.dma_start(out=gain_sb[:], in_=gain.rearrange("(g p t) -> p g t", p=P, t=PACK))
+        for g in range(2, GROUPS):
+            load_w1(g)
+
+        ident = kept("ident", [P, P], F32)
+        make_identity(nc, ident[:])
+        warm = kept("warm", [P, 1], F32)
+        nc.scalar.activation(out=warm[:], in_=ident[:, 0:1], func=SILU)
+
+        emb_codes = kept("emb_codes", [P, T], U32)
+        emb_scales = kept("emb_scales", [P, T], U8)
+        blend_codes = kept("blend_codes", [P, TIME_PASSES, S], U32)
+        blend_scales = kept("blend_scales", [P, TIME_PASSES, S], U8)
+        y_scales = kept("y_scales", [P, S], U8)
+
+        def quantize(codes, scales, values):
+            nc.vector.quantize_mx(out=codes.bitcast(FP8X4), scales=scales, in_=values)
+
+        def turn_rows(raw, h):
+            words = raw[:].bitcast(F32)
+            bank = next_bank()
+            for a in range(2):
+                for u in range(2):
+                    col = (2 * a + u) * P
+                    first = h * 2 * P + u
+                    nc.tensor.transpose(
+                        bank[:, col : col + P], words[:, a, first : (h + 1) * 2 * P : 2], ident[:]
+                    )
+            turned = ring(keep, "turned", 4, [P, 2 * P * PACK], BF16)
+            nc.scalar.copy(
+                out=turned[:].bitcast(F32).rearrange("p (a m u) -> p a m u", a=2, u=2),
+                in_=bank[:].rearrange("p (a u m) -> p a m u", a=2, u=2),
+            )
+            return turned
+
+        def quantize_emb(h, pair, turned):
+            cols = slice((2 * h + pair) * 2 * P, (2 * h + pair + 1) * 2 * P)
+            quantize(emb_codes[:, cols], emb_scales[:, cols], turned[:])
+
+        def quantize_blend(piece, h, turned):
+            cols = slice(piece * PIECE, (piece + 1) * PIECE)
+            quantize(blend_codes[:, h, cols], blend_scales[:, h, cols], turned[:])
+
+        w1_grouped = {}
+        w1_mx = {}
+
+        def interleave_w1(n):
+            g, t = divmod(n, PACK)
+            w1_grouped[n] = ring(keep, "w1_grouped", 3, [P, P * PACK], BF16)
+            nc.vector.tensor_copy(
+                out=w1_grouped[n][:].rearrange("p (m j) -> p m j", j=PACK),
+                in_=w1_raw[g][:].rearrange("p j (m t) -> p t m j", t=PACK)[:, t],
+            )
+
+        def quantize_w1(n):
+            codes = ring(keep, "w1_codes", 6, [P, P], U32)
+            scales = ring(keep, "w1_scales", 6, [P, P], U8)
+            quantize(codes[:], scales[:], w1_grouped[n][:])
+            w1_mx[n] = codes, scales
+
+        hidden = {}
+        z_bf16 = {}
+        z_mx = {}
+
+        def first_stage(n, passes=range(TIME_PASSES)):
+            codes, scales = w1_mx[n]
+            if n not in hidden:
+                hidden[n] = ring(keep, "hidden", 4, [P, TIME_PASSES, P, PACK], F32)
+            for h in passes:
+                bank = next_bank()
+                for t in range(PACK):
+                    cols = slice((h * PACK + t) * P, (h * PACK + t + 1) * P)
+                    nc.tensor.matmul_mx(
+                        out=bank[:, t * P : (t + 1) * P],
+                        lhsT=emb_codes[:, cols].bitcast(FP8X4),
+                        lhsT_scale=emb_scales[:, cols],
+                        rhs=codes[:].bitcast(FP8X4),
+                        rhs_scale=scales[:],
+                        start=True,
+                        stop=True,
+                    )
+                nc.scalar.activation(
+                    out=hidden[n][:, h], in_=bank[:].rearrange("p (t m) -> p m t", t=PACK), func=SILU
+                )
+
+        def scale_hidden(n):
+            z_bf16[n] = ring(keep, "z_bf16", 2, [P, TIME_PASSES, P, PACK], BF16)
+            nc.vector.tensor_tensor(
+                out=z_bf16[n][:],
+                in0=hidden[n][:],
+                in1=scale_sb[:].unsqueeze(2).to_broadcast([P, TIME_PASSES, P, PACK]),
+                op=MULT,
+            )
+
+        def quantize_z(n):
+            codes = ring(keep, "z_codes", 8, [P, TIME_PASSES * P], U32)
+            scales = ring(keep, "z_scales", 8, [P, TIME_PASSES * P], U8)
+            quantize(codes[:], scales[:], z_bf16[n][:].rearrange("p h m t -> p (h m t)"))
+            z_mx[n] = codes, scales
+
+        silu_out = {}
+        y_turned = {}
+        complete = []
+
+        def second_stage(g, slots, start, width):
+            bank = next_bank()
+            rows = slice(start, start + width)
+            for i, t in enumerate(slots):
+                codes, scales = z_mx[g * PACK + t]
+                for h in range(TIME_PASSES):
+                    nc.tensor.matmul_mx(
+                        out=bank[:, i * width : (i + 1) * width],
+                        lhsT=codes[:, h * P : (h + 1) * P].bitcast(FP8X4),
+                        lhsT_scale=scales[:, h * P : (h + 1) * P],
+                        rhs=blend_codes[:, h, rows].bitcast(FP8X4),
+                        rhs_scale=blend_scales[:, h, rows],
+                        start=(h == 0),
+                        stop=(h == TIME_PASSES - 1),
+                    )
+            for i, t in enumerate(slots):
+                silu_out[g, t, start] = ring(keep, "silu_out", 6, [P, width], F32)
+                nc.scalar.activation(
+                    out=silu_out[g, t, start][:],
+                    in_=bank[:, i * width : (i + 1) * width],
+                    func=SILU,
+                    bias=bias_sb[:, g, t : t + 1],
+                )
+
+        def apply_gain(g, t, start, width):
+            if t == PACK - 1:
+                complete.extend((g, piece) for piece in range(start // PIECE, (start + width) // PIECE))
+            if t == 0:
+                y_turned[g, start] = ring(keep, "y_turned%d_" % start, 3, [P, PACK, width], F32)
+            nc.vector.tensor_scalar(
+                out=y_turned[g, start][:, t, :],
+                in0=silu_out[g, t, start][:],
+                scalar1=gain_sb[:, g, t : t + 1],
+                scalar2=None,
+                op0=MULT,
+            )
+
+        def y_window(g, row, count):
+            start = max(s for (h, s) in y_turned if h == g and s <= row)
+            return y_turned[g, start][:, :, row - start : row - start + count]
+
+        def store_y(g, a, copy):
+            source = y_window(g, a * P, P)
+            bank = next_bank()
+            for t in range(PACK):
+                nc.tensor.transpose(bank[:, t * P : (t + 1) * P], source[:, t, :], ident[:])
+            rows = ring(keep, "y_rows", 6, [P, K_PASS], F32)
+            copy(
+                out=rows[:].rearrange("s (p t) -> s p t", t=PACK),
+                in_=bank[:].rearrange("s (t p) -> s p t", t=PACK),
+            )
+            nc.sync.dma_start(
+                out=out_0[a * P : (a + 1) * P, g * K_PASS : (g + 1) * K_PASS], in_=rows[:]
+            )
+
+        y_bf16 = {}
+        y_codes = {}
+
+        def round_y(g, piece):
+            y_bf16[g, piece] = ring(keep, "y_bf16", 2, [P, PIECE * PACK], BF16)
+            nc.vector.tensor_copy(
+                out=y_bf16[g, piece][:].rearrange("p (c i t) -> p c t i", i=4, t=PACK),
+                in_=y_window(g, piece * PIECE, PIECE).rearrange("p t (c i) -> p c t i", i=4),
+            )
+
+        def quantize_y(g, piece):
+            cols = slice(piece * PIECE, (piece + 1) * PIECE)
+            codes = ring(keep, "y_codes", 6, [P, PIECE], U32)
+            quantize(codes[:], y_scales[PACK * g :, cols], y_bf16[g, piece][:])
+            y_codes[g, piece] = codes
+
+        def store_codes(g, piece):
+            cols = slice(piece * PIECE, (piece + 1) * PIECE)
+            words = out_1[g].rearrange("p m t -> p (m t)").bitcast(I32)
+            nc.sync.dma_start(out=words[:, cols], in_=y_codes[g, piece][:].bitcast(I32))
+
+        on_scalar, on_vector = nc.scalar.copy, nc.vector.tensor_copy
+        turned = [turn_rows(emb_raw[h, pair], 0) for h in range(TIME_PASSES) for pair in range(2)]
+        quantize_emb(0, 0, turned[0])
+        interleave_w1(0)
+        quantize_emb(0, 1, turned[1])
+        quantize_w1(0)
+        interleave_w1(1)
+        quantize_emb(1, 0, turned[2])
+        quantize_w1(1)
+        interleave_w1(2)
+        quantize_emb(1, 1, turned[3])
+        quantize_w1(2)
+        interleave_w1(3)
+        last = GROUPS - 1
+        planes = [(g, piece) for g in range(GROUPS) for piece in range(PIECES)]
+        rounded, quantized, stored = [], [], []
+
+        def advance_planes():
+            if len(stored) < len(quantized):
+                stored.append(quantized[len(stored)])
+                store_codes(*stored[-1])
+            if len(quantized) < len(rounded):
+                quantized.append(rounded[len(quantized)])
+                quantize_y(*quantized[-1])
+            if len(rounded) < len(complete):
+                rounded.append(complete[len(rounded)])
+                round_y(*rounded[-1])
+
+        for step in range(UNITS):
+            g, k = divmod(step - PACK, PACK)
+            first_stage(step)
+            blend_turned = []
+            if g < 0 and k >= 1:
+                blend_turned = [turn_rows(blend_raw[k - 1], h) for h in range(TIME_PASSES)]
+            gains = []
+            if g >= 0 and k < 2:
+                for t in (2 * k, 2 * k + 1):
+                    second_stage(g, [t], 0, WIDE)
+                    gains.append((g, t, 0, WIDE))
+            elif g >= 0:
+                slots = [2 * k - 4, 2 * k - 3]
+                second_stage(g, slots, WIDE, NARROW)
+                gains = [(g, t, WIDE, NARROW) for t in slots]
+            if step + 3 < UNITS:
+                quantize_w1(step + 3)
+            scale_hidden(step)
+            for args in gains:
+                apply_gain(*args)
+            if step + 4 < UNITS:
+                interleave_w1(step + 4)
+            quantize_z(step)
+            for h, values in enumerate(blend_turned):
+                quantize_blend(k - 1, h, values)
+            if g >= 0 and k >= 2:
+                store_y(g, 2 * k - 4, on_scalar)
+                store_y(g, 2 * k - 3, on_scalar)
+            if g >= 1 and k < 2:
+                store_y(g - 1, 4 + k, on_scalar)
+            if step >= 8 and k != 3:
+                advance_planes()
+
+        for piece in range(PIECES):
+            start = piece * PIECE
+            for i, slots in enumerate(([0, 1], [2, 3])):
+                second_stage(last, slots, start, PIECE)
+                if piece == 0:
+                    store_y(last - 1, 4 + i, on_scalar)
+                advance_planes()
+                for t in slots:
+                    apply_gain(last, t, start, PIECE)
+            if piece > 0:
+                store_y(last, 2 * piece - 2, on_scalar)
+                store_y(last, 2 * piece - 1, on_scalar)
+        while len(rounded) < len(complete):
+            advance_planes()
+        store_y(last, 2 * PIECES - 2, on_scalar)
+        advance_planes()
+        store_y(last, 2 * PIECES - 1, on_scalar)
+        while len(stored) < len(complete):
+            advance_planes()
+
+        scale_words = out_2.bitcast(I32)
+        for q in range(4):
+            nc.sync.dma_start(
+                out=scale_words[:, PACK * q : PACK * q + PACK, :],
+                in_=y_scales[32 * q : 32 * q + PACK * GROUPS, :].bitcast(I32),
+            )

@@ -62,10 +62,10 @@ def tile_timestep_blend_conditioning_h3_kernel(
             emb_raw[h, pair] = kept("emb_raw%d_%d" % (h, pair), [P, 2, D], BF16)
             nc.sync.dma_start(out=emb_raw[h, pair][:], in_=emb_rows[h, :, 2 * pair : 2 * pair + 2, :])
 
-        def load_w1(g):
-            w1_raw[g] = kept("w1_raw%d" % g, [P, PACK, K_PASS], BF16)
-            cols = w1[:, g * K_PASS : (g + 1) * K_PASS]
-            nc.sync.dma_start(out=w1_raw[g][:], in_=cols.rearrange("(p j) c -> p j c", j=PACK))
+        def load_w1(g, start=0, width=K_PASS):
+            w1_raw[g, start] = kept("w1_raw%d_%d" % (g, start), [P, PACK, width], BF16)
+            cols = w1[:, g * K_PASS + start : g * K_PASS + start + width]
+            nc.sync.dma_start(out=w1_raw[g, start][:], in_=cols.rearrange("(p j) c -> p j c", j=PACK))
 
         def load_blend(piece):
             blend_raw[piece] = kept("blend_raw%d" % piece, [P, 2, T], BF16)
@@ -74,15 +74,16 @@ def tile_timestep_blend_conditioning_h3_kernel(
 
         load_emb(0, 0)
         load_emb(0, 1)
-        load_w1(0)
+        load_w1(0, 0, 2 * P)
         load_emb(1, 0)
         load_emb(1, 1)
+        load_w1(0, 2 * P, K_PASS - 2 * P)
         scale_sb = kept("scale_sb", [P, TIME_PASSES, PACK], BF16)
         bias_sb = kept("bias_sb", [P, GROUPS, PACK], BF16)
         gain_sb = kept("gain_sb", [P, GROUPS, PACK], BF16)
         nc.scalar.dma_start(out=scale_sb[:], in_=time_scale.rearrange("(h p t) -> p h t", p=P, t=PACK))
-        load_blend(0)
         load_w1(1)
+        load_blend(0)
         load_blend(1)
         load_blend(2)
         nc.sync.dma_start(out=bias_sb[:], in_=bias.rearrange("(g p t) -> p g t", p=P, t=PACK))
@@ -95,6 +96,7 @@ def tile_timestep_blend_conditioning_h3_kernel(
         warm = kept("warm", [P, 1], F32)
         nc.scalar.activation(out=warm[:], in_=ident[:, 0:1], func=SILU)
 
+        scale_view = scale_sb[:]
         emb_codes = kept("emb_codes", [P, T], U32)
         emb_scales = kept("emb_scales", [P, T], U8)
         blend_codes = kept("blend_codes", [P, TIME_PASSES, S], U32)
@@ -132,28 +134,37 @@ def tile_timestep_blend_conditioning_h3_kernel(
         w1_grouped = {}
         w1_mx = {}
 
-        def interleave_w1(n):
-            g, t = divmod(n, PACK)
-            w1_grouped[n] = ring(keep, "w1_grouped", 3, [P, P * PACK], BF16)
+        def interleave_w1(g, start, width):
+            base = max(b for (h, b) in w1_raw if h == g and b <= start)
+            if start == 0:
+                w1_grouped[g] = ring(keep, "w1_grouped", 2, [P, K_PASS * PACK], BF16)
             nc.vector.tensor_copy(
-                out=w1_grouped[n][:].rearrange("p (m j) -> p m j", j=PACK),
-                in_=w1_raw[g][:].rearrange("p j (m t) -> p t m j", t=PACK)[:, t],
+                out=w1_grouped[g][:, start * PACK : (start + width) * PACK].rearrange(
+                    "p (c i j) -> p c j i", i=4, j=PACK
+                ),
+                in_=w1_raw[g, base][:, :, start - base : start - base + width].rearrange("p j (c i) -> p c j i", i=4),
             )
 
-        def quantize_w1(n):
-            codes = ring(keep, "w1_codes", 6, [P, P], U32)
-            scales = ring(keep, "w1_scales", 6, [P, P], U8)
-            quantize(codes[:], scales[:], w1_grouped[n][:])
-            w1_mx[n] = codes, scales
+        def quantize_w1(g, start, width):
+            if start == 0:
+                w1_mx[g] = (
+                    ring(keep, "w1_codes", 2, [P, K_PASS], U32),
+                    ring(keep, "w1_scales", 2, [P, K_PASS], U8),
+                )
+            codes, scales = w1_mx[g]
+            cols = slice(start, start + width)
+            quantize(codes[:, cols], scales[:, cols], w1_grouped[g][:, start * PACK : (start + width) * PACK])
 
         hidden = {}
         z_bf16 = {}
         z_mx = {}
 
         def first_stage(n, passes=range(TIME_PASSES)):
-            codes, scales = w1_mx[n]
+            g, c = divmod(n, PACK)
+            codes, scales = w1_mx[g]
+            feats = slice(c * P, (c + 1) * P)
             if n not in hidden:
-                hidden[n] = ring(keep, "hidden", 4, [P, TIME_PASSES, P, PACK], F32)
+                hidden[n] = ring(keep, "hidden", 4, [P, TIME_PASSES, PACK, P // PACK, PACK], F32)
             for h in passes:
                 bank = next_bank()
                 for t in range(PACK):
@@ -162,29 +173,39 @@ def tile_timestep_blend_conditioning_h3_kernel(
                         out=bank[:, t * P : (t + 1) * P],
                         lhsT=emb_codes[:, cols].bitcast(FP8X4),
                         lhsT_scale=emb_scales[:, cols],
-                        rhs=codes[:].bitcast(FP8X4),
-                        rhs_scale=scales[:],
+                        rhs=codes[:, feats].bitcast(FP8X4),
+                        rhs_scale=scales[:, feats],
                         start=True,
                         stop=True,
                     )
                 nc.scalar.activation(
-                    out=hidden[n][:, h], in_=bank[:].rearrange("p (t m) -> p m t", t=PACK), func=SILU
+                    out=hidden[n][:, h],
+                    in_=bank[:].rearrange("p (t m s) -> p s m t", t=PACK, s=PACK),
+                    func=SILU,
                 )
 
         def scale_hidden(n):
-            z_bf16[n] = ring(keep, "z_bf16", 2, [P, TIME_PASSES, P, PACK], BF16)
+            g, c = divmod(n, PACK)
+            if c == 0:
+                z_bf16[g] = ring(keep, "z_bf16", 2, [P, PACK, TIME_PASSES, P, PACK], BF16)
+            quarter = P // PACK
             nc.vector.tensor_tensor(
-                out=z_bf16[n][:],
-                in0=hidden[n][:],
-                in1=scale_sb[:].unsqueeze(2).to_broadcast([P, TIME_PASSES, P, PACK]),
+                out=z_bf16[g][:, :, :, c * quarter : (c + 1) * quarter, :].rearrange("p s h m t -> p h s (m t)"),
+                in0=hidden[n][:].rearrange("p h s m t -> p h (s m) t"),
+                in1=scale_view.unsqueeze(2).to_broadcast([P, TIME_PASSES, P, PACK]),
                 op=MULT,
             )
 
-        def quantize_z(n):
-            codes = ring(keep, "z_codes", 8, [P, TIME_PASSES * P], U32)
-            scales = ring(keep, "z_scales", 8, [P, TIME_PASSES * P], U8)
-            quantize(codes[:], scales[:], z_bf16[n][:].rearrange("p h m t -> p (h m t)"))
-            z_mx[n] = codes, scales
+        def quantize_z(g, half):
+            codes = ring(keep, "z_codes", 4, [P, 2, TIME_PASSES * P], U32)
+            scales = ring(keep, "z_scales", 4, [P, 2, TIME_PASSES * P], U8)
+            quantize(
+                codes[:].rearrange("p s w -> p (s w)"),
+                scales[:].rearrange("p s w -> p (s w)"),
+                z_bf16[g][:, 2 * half : 2 * half + 2].rearrange("p s h m t -> p (s h m t)"),
+            )
+            for i in range(2):
+                z_mx[g * PACK + 2 * half + i] = codes[:, i, :], scales[:, i, :]
 
         silu_out = {}
         y_turned = {}
@@ -206,9 +227,10 @@ def tile_timestep_blend_conditioning_h3_kernel(
                         stop=(h == TIME_PASSES - 1),
                     )
             for i, t in enumerate(slots):
-                silu_out[g, t, start] = ring(keep, "silu_out", 6, [P, width], F32)
+                if (g, t) not in silu_out:
+                    silu_out[g, t] = ring(keep, "silu_out", 6, [P, S], F32)
                 nc.scalar.activation(
-                    out=silu_out[g, t, start][:],
+                    out=silu_out[g, t][:, rows],
                     in_=bank[:, i * width : (i + 1) * width],
                     func=SILU,
                     bias=bias_sb[:, g, t : t + 1],
@@ -218,10 +240,10 @@ def tile_timestep_blend_conditioning_h3_kernel(
             if t == PACK - 1:
                 complete.extend((g, piece) for piece in range(start // PIECE, (start + width) // PIECE))
             if t == 0:
-                y_turned[g, start] = ring(keep, "y_turned%d_" % start, 3, [P, PACK, width], F32)
+                y_turned[g, start] = ring(keep, "y_turned%d_%d_%d" % (start, width, g == GROUPS - 1), 1 if g == GROUPS - 1 else 2, [P, PACK, width], F32)
             nc.vector.tensor_scalar(
                 out=y_turned[g, start][:, t, :],
-                in0=silu_out[g, t, start][:],
+                in0=silu_out[g, t][:, start : start + width],
                 scalar1=gain_sb[:, g, t : t + 1],
                 scalar2=None,
                 op0=MULT,
@@ -248,11 +270,23 @@ def tile_timestep_blend_conditioning_h3_kernel(
         y_bf16 = {}
         y_codes = {}
 
-        def round_y(g, piece):
+        def round_y(g, piece, on_gpsimd):
+            source = y_window(g, piece * PIECE, PIECE)
+            if on_gpsimd:
+                y_bf16[g, piece] = ring(keep, "y_bf16_g", 1, [P, PIECE * PACK], BF16)
+                nc.gpsimd.tensor_scalar(
+                    out=y_bf16[g, piece][:].rearrange("p (m t) -> p m t", t=PACK),
+                    in0=source.rearrange("p t m -> p m t"),
+                    scalar1=1.0,
+                    scalar2=1.0,
+                    op0=MULT,
+                    op1=MULT,
+                )
+                return
             y_bf16[g, piece] = ring(keep, "y_bf16", 2, [P, PIECE * PACK], BF16)
             nc.vector.tensor_copy(
                 out=y_bf16[g, piece][:].rearrange("p (c i t) -> p c t i", i=4, t=PACK),
-                in_=y_window(g, piece * PIECE, PIECE).rearrange("p t (c i) -> p c t i", i=4),
+                in_=source.rearrange("p t (c i) -> p c t i", i=4),
             )
 
         def quantize_y(g, piece):
@@ -269,21 +303,19 @@ def tile_timestep_blend_conditioning_h3_kernel(
         on_scalar, on_vector = nc.scalar.copy, nc.vector.tensor_copy
         turned = [turn_rows(emb_raw[h, pair], 0) for h in range(TIME_PASSES) for pair in range(2)]
         quantize_emb(0, 0, turned[0])
-        interleave_w1(0)
+        interleave_w1(0, 0, 2 * P)
         quantize_emb(0, 1, turned[1])
-        quantize_w1(0)
-        interleave_w1(1)
+        quantize_w1(0, 0, 2 * P)
         quantize_emb(1, 0, turned[2])
-        quantize_w1(1)
-        interleave_w1(2)
         quantize_emb(1, 1, turned[3])
-        quantize_w1(2)
-        interleave_w1(3)
+        interleave_w1(0, 2 * P, 2 * P)
+        interleave_w1(1, 0, K_PASS)
+        quantize_w1(0, 2 * P, 2 * P)
+
         last = GROUPS - 1
-        planes = [(g, piece) for g in range(GROUPS) for piece in range(PIECES)]
         rounded, quantized, stored = [], [], []
 
-        def advance_planes():
+        def advance_planes(on_gpsimd):
             if len(stored) < len(quantized):
                 stored.append(quantized[len(stored)])
                 store_codes(*stored[-1])
@@ -292,60 +324,54 @@ def tile_timestep_blend_conditioning_h3_kernel(
                 quantize_y(*quantized[-1])
             if len(rounded) < len(complete):
                 rounded.append(complete[len(rounded)])
-                round_y(*rounded[-1])
+                round_y(*rounded[-1], on_gpsimd)
 
-        for step in range(UNITS):
-            g, k = divmod(step - PACK, PACK)
-            first_stage(step)
-            blend_turned = []
-            if g < 0 and k >= 1:
-                blend_turned = [turn_rows(blend_raw[k - 1], h) for h in range(TIME_PASSES)]
-            gains = []
-            if g >= 0 and k < 2:
-                for t in (2 * k, 2 * k + 1):
-                    second_stage(g, [t], 0, WIDE)
-                    gains.append((g, t, 0, WIDE))
-            elif g >= 0:
-                slots = [2 * k - 4, 2 * k - 3]
-                second_stage(g, slots, WIDE, NARROW)
-                gains = [(g, t, WIDE, NARROW) for t in slots]
-            if step + 3 < UNITS:
-                quantize_w1(step + 3)
-            scale_hidden(step)
-            for args in gains:
+        wide = [([0], 0, WIDE), ([1], 0, WIDE), ([2], 0, WIDE), ([3], 0, WIDE), ([0, 1], WIDE, NARROW), ([2, 3], WIDE, NARROW)]
+        narrow = [(slots, piece * PIECE, PIECE) for piece in range(PIECES) for slots in ([0, 1], [2, 3])]
+        products = [(PACK * g + PACK + 1, g) + b for g in range(GROUPS) for b in (wide if g < last else narrow)]
+        pattern = ["sts", "tst", "sts", "tst"]
+        pending, tiles = [], []
+        done = 0
+        step = 0
+        while done < GROUPS * S // P:
+            k = step % PACK
+            if step < UNITS:
+                first_stage(step)
+            for args in pending:
                 apply_gain(*args)
-            if step + 4 < UNITS:
-                interleave_w1(step + 4)
-            quantize_z(step)
-            for h, values in enumerate(blend_turned):
-                quantize_blend(k - 1, h, values)
-            if g >= 0 and k >= 2:
-                store_y(g, 2 * k - 4, on_scalar)
-                store_y(g, 2 * k - 3, on_scalar)
-            if g >= 1 and k < 2:
-                store_y(g - 1, 4 + k, on_scalar)
-            if step >= 8 and k != 3:
-                advance_planes()
-
-        for piece in range(PIECES):
-            start = piece * PIECE
-            for i, slots in enumerate(([0, 1], [2, 3])):
-                second_stage(last, slots, start, PIECE)
-                if piece == 0:
-                    store_y(last - 1, 4 + i, on_scalar)
-                advance_planes()
-                for t in slots:
-                    apply_gain(last, t, start, PIECE)
-            if piece > 0:
-                store_y(last, 2 * piece - 2, on_scalar)
-                store_y(last, 2 * piece - 1, on_scalar)
-        while len(rounded) < len(complete):
-            advance_planes()
-        store_y(last, 2 * PIECES - 2, on_scalar)
-        advance_planes()
-        store_y(last, 2 * PIECES - 1, on_scalar)
+                if args[1] == PACK - 1:
+                    for a in range(args[2] // P, (args[2] + args[3]) // P):
+                        tiles.append((step + 1, args[0], a))
+            pending = []
+            if 2 <= step <= PIECES + 1:
+                for h, values in enumerate(blend_turned):
+                    quantize_blend(step - 2, h, values)
+            if k == 0 and 0 < step <= UNITS:
+                quantize_z(step // PACK - 1, 0)
+                quantize_z(step // PACK - 1, 1)
+            if k == 1 and 0 < step // PACK < last:
+                interleave_w1(step // PACK + 1, 0, K_PASS)
+            if k == 2 and step // PACK < last:
+                quantize_w1(step // PACK + 1, 0, K_PASS)
+            if step >= 10 and (k != 0 or step >= UNITS):
+                advance_planes(False)
+            if step > UNITS:
+                advance_planes(False)
+            if step < UNITS:
+                scale_hidden(step)
+            if 1 <= step <= PIECES:
+                blend_turned = [turn_rows(blend_raw[step - 1], h) for h in range(TIME_PASSES)]
+            for i, item in enumerate(pattern[k] if step < UNITS else "tstst"):
+                if item == "s" and products and products[0][0] <= step:
+                    g, slots, start, width = products.pop(0)[1:]
+                    second_stage(g, slots, start, width)
+                    pending.extend((g, t, start, width) for t in slots)
+                if item == "t" and tiles and tiles[0][0] <= step:
+                    store_y(*tiles.pop(0)[1:], on_vector if (False) else on_scalar)
+                    done = done + 1
+            step = step + 1
         while len(stored) < len(complete):
-            advance_planes()
+            advance_planes(False)
 
         scale_words = out_2.bitcast(I32)
         for q in range(4):

@@ -19,7 +19,7 @@ P = 128
 PACK = 4
 K_PASS = P * PACK
 BANK = 512
-BANKS = 8
+BANKS = 7
 TIME_PASSES = T // K_PASS
 GROUPS = F // K_PASS
 UNITS = GROUPS * PACK
@@ -78,25 +78,33 @@ def tile_timestep_blend_conditioning_h3_kernel(
         load_emb(1, 0)
         load_emb(1, 1)
         load_w1(0, 2 * P, K_PASS - 2 * P)
-        scale_sb = kept("scale_sb", [P, TIME_PASSES, PACK], BF16)
+        scale_rows = kept("scale_rows", [TIME_PASSES, K_PASS], BF16)
         bias_sb = kept("bias_sb", [P, GROUPS, PACK], BF16)
         gain_sb = kept("gain_sb", [P, GROUPS, PACK], BF16)
-        nc.scalar.dma_start(out=scale_sb[:], in_=time_scale.rearrange("(h p t) -> p h t", p=P, t=PACK))
+        nc.scalar.dma_start(out=scale_rows[:], in_=time_scale.rearrange("(h k) -> h k", h=TIME_PASSES))
         load_w1(1)
         load_blend(0)
+        load_w1(2)
         load_blend(1)
         load_blend(2)
         nc.sync.dma_start(out=bias_sb[:], in_=bias.rearrange("(g p t) -> p g t", p=P, t=PACK))
         nc.sync.dma_start(out=gain_sb[:], in_=gain.rearrange("(g p t) -> p g t", p=P, t=PACK))
-        for g in range(2, GROUPS):
-            load_w1(g)
+        load_w1(3)
 
         ident = kept("ident", [P, P], F32)
         make_identity(nc, ident[:])
         warm = kept("warm", [P, 1], F32)
         nc.scalar.activation(out=warm[:], in_=ident[:, 0:1], func=SILU)
 
-        scale_view = scale_sb[:]
+        scale_sorted = kept("scale_sorted", [P, K_PASS], F32)
+        nc.vector.memset(scale_sorted[:], 0.0)
+        nc.vector.tensor_copy(
+            out=scale_sorted[0:TIME_PASSES, :].rearrange("h (t p) -> h t p", t=PACK),
+            in_=scale_rows[:].rearrange("h (p t) -> h t p", t=PACK),
+        )
+        scale_bank = psum.tile([P, BANK], F32, name="scale_bank", tag="scale_bank")
+        scale_view = scale_bank[:].rearrange("p (t h) -> p h t", t=PACK)[:, 0:TIME_PASSES, :]
+
         emb_codes = kept("emb_codes", [P, T], U32)
         emb_scales = kept("emb_scales", [P, T], U8)
         blend_codes = kept("blend_codes", [P, TIME_PASSES, S], U32)
@@ -134,26 +142,34 @@ def tile_timestep_blend_conditioning_h3_kernel(
         w1_grouped = {}
         w1_mx = {}
 
-        def interleave_w1(g, start, width):
-            base = max(b for (h, b) in w1_raw if h == g and b <= start)
-            if start == 0:
-                w1_grouped[g] = ring(keep, "w1_grouped", 2, [P, K_PASS * PACK], BF16)
-            nc.vector.tensor_copy(
-                out=w1_grouped[g][:, start * PACK : (start + width) * PACK].rearrange(
-                    "p (c i j) -> p c j i", i=4, j=PACK
-                ),
-                in_=w1_raw[g, base][:, :, start - base : start - base + width].rearrange("p j (c i) -> p c j i", i=4),
-            )
+        def pool_copy(out, in_):
+            nc.gpsimd.tensor_scalar(out=out, in0=in_, scalar1=1.0, scalar2=1.0, op0=MULT, op1=MULT)
 
-        def quantize_w1(g, start, width):
-            if start == 0:
+        def interleave_w1(g, half, on_gpsimd):
+            base = max(b for (h, b) in w1_raw if h == g and b <= half * PIECE)
+            source = w1_raw[g, base][:, :, half * PIECE - base : (half + 1) * PIECE - base]
+            if g == 0:
+                values = ring(keep, "w1_first", 2, [P, PIECE * PACK], BF16)
+            else:
+                values = ring(keep, "staged", 2, [P, PIECE * PACK], BF16)
+            w1_grouped[g, half] = values
+            if on_gpsimd:
+                pool_copy(values[:].rearrange("p (c j) -> p c j", j=PACK), source.rearrange("p j c -> p c j"))
+            else:
+                nc.vector.tensor_copy(
+                    out=values[:].rearrange("p (c i j) -> p c j i", i=4, j=PACK),
+                    in_=source.rearrange("p j (c i) -> p c j i", i=4),
+                )
+
+        def quantize_w1(g, half):
+            if half == 0:
                 w1_mx[g] = (
                     ring(keep, "w1_codes", 2, [P, K_PASS], U32),
                     ring(keep, "w1_scales", 2, [P, K_PASS], U8),
                 )
             codes, scales = w1_mx[g]
-            cols = slice(start, start + width)
-            quantize(codes[:, cols], scales[:, cols], w1_grouped[g][:, start * PACK : (start + width) * PACK])
+            cols = slice(half * PIECE, (half + 1) * PIECE)
+            quantize(codes[:, cols], scales[:, cols], w1_grouped[g, half][:])
 
         hidden = {}
         z_bf16 = {}
@@ -163,8 +179,8 @@ def tile_timestep_blend_conditioning_h3_kernel(
             g, c = divmod(n, PACK)
             codes, scales = w1_mx[g]
             feats = slice(c * P, (c + 1) * P)
-            if n not in hidden:
-                hidden[n] = ring(keep, "hidden", 4, [P, TIME_PASSES, PACK, P // PACK, PACK], F32)
+            if n % 2 == 0:
+                hidden[n // 2] = ring(keep, "hidden", 2, [P, TIME_PASSES, PACK, 2, P // PACK, PACK], F32)
             for h in passes:
                 bank = next_bank()
                 for t in range(PACK):
@@ -179,20 +195,20 @@ def tile_timestep_blend_conditioning_h3_kernel(
                         stop=True,
                     )
                 nc.scalar.activation(
-                    out=hidden[n][:, h],
+                    out=hidden[n // 2][:, h, :, n % 2],
                     in_=bank[:].rearrange("p (t m s) -> p s m t", t=PACK, s=PACK),
                     func=SILU,
                 )
 
-        def scale_hidden(n):
-            g, c = divmod(n, PACK)
+        def scale_hidden(pair):
+            g, c = divmod(pair, 2)
             if c == 0:
                 z_bf16[g] = ring(keep, "z_bf16", 2, [P, PACK, TIME_PASSES, P, PACK], BF16)
-            quarter = P // PACK
+            half = P // 2
             nc.vector.tensor_tensor(
-                out=z_bf16[g][:, :, :, c * quarter : (c + 1) * quarter, :].rearrange("p s h m t -> p h s (m t)"),
-                in0=hidden[n][:].rearrange("p h s m t -> p h (s m) t"),
-                in1=scale_view.unsqueeze(2).to_broadcast([P, TIME_PASSES, P, PACK]),
+                out=z_bf16[g][:, :, :, c * half : (c + 1) * half, :].rearrange("p s h m t -> p h s (m t)"),
+                in0=hidden[pair][:].rearrange("p h s c m t -> p h (s c m) t"),
+                in1=scale_view.unsqueeze(2).to_broadcast([P, TIME_PASSES, 2 * P, PACK]),
                 op=MULT,
             )
 
@@ -237,12 +253,12 @@ def tile_timestep_blend_conditioning_h3_kernel(
                 )
 
         def apply_gain(g, t, start, width):
-            if t == PACK - 1:
+            if t == PACK - 1 and g >= 2:
                 complete.extend((g, piece) for piece in range(start // PIECE, (start + width) // PIECE))
-            if t == 0:
-                y_turned[g, start] = ring(keep, "y_turned%d_%d_%d" % (start, width, g == GROUPS - 1), 1 if g == GROUPS - 1 else 2, [P, PACK, width], F32)
+            if g not in y_turned:
+                y_turned[g] = ring(keep, "y_turned", 3, [P, PACK, S], F32)
             nc.vector.tensor_scalar(
-                out=y_turned[g, start][:, t, :],
+                out=y_turned[g][:, t, start : start + width],
                 in0=silu_out[g, t][:, start : start + width],
                 scalar1=gain_sb[:, g, t : t + 1],
                 scalar2=None,
@@ -250,23 +266,55 @@ def tile_timestep_blend_conditioning_h3_kernel(
             )
 
         def y_window(g, row, count):
-            start = max(s for (h, s) in y_turned if h == g and s <= row)
-            return y_turned[g, start][:, :, row - start : row - start + count]
+            return y_turned[g][:, :, row : row + count]
 
-        def store_y(g, a, copy):
+        HALF = S // 2
+        y_half = {}
+        half_codes = {}
+
+        def round_half(g, half):
+            y_half[g, half] = ring(keep, "staged", 2, [P, HALF * PACK], BF16)
+            pool_copy(
+                y_half[g, half][:].rearrange("p (m t) -> p m t", t=PACK),
+                y_window(g, half * HALF, HALF).rearrange("p t m -> p m t"),
+            )
+
+        def quantize_half(g, half):
+            codes = ring(keep, "y_half_codes", 2, [P, HALF], U32)
+            for start, width in ((0, PIECE), (PIECE, HALF - PIECE)):
+                cols = slice(half * HALF + start, half * HALF + start + width)
+                values = y_half[g, half][:, start * PACK : (start + width) * PACK]
+                quantize(codes[:, start : start + width], y_scales[PACK * g :, cols], values)
+            half_codes[g, half] = codes
+
+        def store_half(g, half):
+            words = out_1[g].rearrange("p m t -> p (m t)").bitcast(I32)
+            nc.sync.dma_start(
+                out=words[:, half * HALF : (half + 1) * HALF], in_=half_codes[g, half][:].bitcast(I32)
+            )
+
+        def store_y(g, a, late_copy):
             source = y_window(g, a * P, P)
             bank = next_bank()
             for t in range(PACK):
                 nc.tensor.transpose(bank[:, t * P : (t + 1) * P], source[:, t, :], ident[:])
-            rows = ring(keep, "y_rows", 6, [P, K_PASS], F32)
-            copy(
-                out=rows[:].rearrange("s (p t) -> s p t", t=PACK),
-                in_=bank[:].rearrange("s (t p) -> s p t", t=PACK),
-            )
-            nc.sync.dma_start(
-                out=out_0[a * P : (a + 1) * P, g * K_PASS : (g + 1) * K_PASS], in_=rows[:]
-            )
 
+            def finish(copy):
+                rows = ring(keep, "y_rows", 6, [P, K_PASS], F32)
+                copy(
+                    out=rows[:].rearrange("s (p t) -> s p t", t=PACK),
+                    in_=bank[:].rearrange("s (t p) -> s p t", t=PACK),
+                )
+                nc.sync.dma_start(
+                    out=out_0[a * P : (a + 1) * P, g * K_PASS : (g + 1) * K_PASS], in_=rows[:]
+                )
+
+            if late_copy:
+                finish(nc.vector.tensor_copy)
+            else:
+                finish(nc.scalar.copy)
+
+        late = []
         y_bf16 = {}
         y_codes = {}
 
@@ -302,15 +350,18 @@ def tile_timestep_blend_conditioning_h3_kernel(
 
         on_scalar, on_vector = nc.scalar.copy, nc.vector.tensor_copy
         turned = [turn_rows(emb_raw[h, pair], 0) for h in range(TIME_PASSES) for pair in range(2)]
+        for t in range(PACK):
+            nc.tensor.transpose(scale_bank[:, t * P : (t + 1) * P], scale_sorted[:, t * P : (t + 1) * P], ident[:])
         quantize_emb(0, 0, turned[0])
-        interleave_w1(0, 0, 2 * P)
+        interleave_w1(0, 0, False)
         quantize_emb(0, 1, turned[1])
-        quantize_w1(0, 0, 2 * P)
+        quantize_w1(0, 0)
         quantize_emb(1, 0, turned[2])
         quantize_emb(1, 1, turned[3])
-        interleave_w1(0, 2 * P, 2 * P)
-        interleave_w1(1, 0, K_PASS)
-        quantize_w1(0, 2 * P, 2 * P)
+        interleave_w1(0, 1, False)
+        interleave_w1(1, 0, False)
+        quantize_w1(0, 1)
+        interleave_w1(1, 1, False)
 
         last = GROUPS - 1
         rounded, quantized, stored = [], [], []
@@ -328,15 +379,18 @@ def tile_timestep_blend_conditioning_h3_kernel(
 
         wide = [([0], 0, WIDE), ([1], 0, WIDE), ([2], 0, WIDE), ([3], 0, WIDE), ([0, 1], WIDE, NARROW), ([2, 3], WIDE, NARROW)]
         narrow = [(slots, piece * PIECE, PIECE) for piece in range(PIECES) for slots in ([0, 1], [2, 3])]
-        products = [(PACK * g + PACK + 1, g) + b for g in range(GROUPS) for b in (wide if g < last else narrow)]
+        products = [(PACK * g + PACK + 2, g) + b for g in range(GROUPS) for b in (wide if g < last else narrow)]
         pattern = ["sts", "tst", "sts", "tst"]
         pending, tiles = [], []
         done = 0
         step = 0
-        while done < GROUPS * S // P:
+        while step < UNITS:
             k = step % PACK
             if step < UNITS:
                 first_stage(step)
+            if k == 0 and 0 < step <= UNITS:
+                quantize_z(step // PACK - 1, 0)
+                quantize_z(step // PACK - 1, 1)
             for args in pending:
                 apply_gain(*args)
                 if args[1] == PACK - 1:
@@ -346,19 +400,27 @@ def tile_timestep_blend_conditioning_h3_kernel(
             if 2 <= step <= PIECES + 1:
                 for h, values in enumerate(blend_turned):
                     quantize_blend(step - 2, h, values)
-            if k == 0 and 0 < step <= UNITS:
-                quantize_z(step // PACK - 1, 0)
-                quantize_z(step // PACK - 1, 1)
-            if k == 1 and 0 < step // PACK < last:
-                interleave_w1(step // PACK + 1, 0, K_PASS)
-            if k == 2 and step // PACK < last:
-                quantize_w1(step // PACK + 1, 0, K_PASS)
-            if step >= 10 and (k != 0 or step >= UNITS):
+            if step % 2 == 1 and step < UNITS:
+                j = step // 2
+                if j < 6:
+                    quantize_w1(1 + j // 2, j % 2)
+                else:
+                    quantize_half(0, j - 6)
+                if j < 4:
+                    interleave_w1(2 + j // 2, j % 2, True)
+                else:
+                    round_half((j - 4) // 2, j % 2)
+                scale_hidden(j)
+            if step in (14, 16):
+                store_half(0, (step - 14) // 2)
+            if step in (16, 17):
+                quantize_half(1, step - 16)
+            if step in (17, 18):
+                store_half(1, step - 17)
+            if step >= UNITS:
                 advance_planes(False)
             if step > UNITS:
                 advance_planes(False)
-            if step < UNITS:
-                scale_hidden(step)
             if 1 <= step <= PIECES:
                 blend_turned = [turn_rows(blend_raw[step - 1], h) for h in range(TIME_PASSES)]
             for i, item in enumerate(pattern[k] if step < UNITS else "tstst"):
@@ -367,11 +429,97 @@ def tile_timestep_blend_conditioning_h3_kernel(
                     second_stage(g, slots, start, width)
                     pending.extend((g, t, start, width) for t in slots)
                 if item == "t" and tiles and tiles[0][0] <= step:
-                    store_y(*tiles.pop(0)[1:], on_vector if (False) else on_scalar)
+                    store_y(*tiles.pop(0)[1:], (step % 2 == 1 and i == 2) if step < UNITS else (False))
                     done = done + 1
             step = step + 1
-        while len(stored) < len(complete):
-            advance_planes(False)
+        quantize_z(last, 0)
+        quantize_z(last, 1)
+        for args in pending[:1]:
+            apply_gain(*args)
+        pending = pending[1:]
+        store_y(1, 3, False)
+        store_half(0, 1)
+        g, slots, start, width = products.pop(0)[1:]
+        second_stage(g, slots, start, width)
+        pending.extend((g, t, start, width) for t in slots)
+        store_y(1, 4, False)
+        g, slots, start, width = products.pop(0)[1:]
+        second_stage(g, slots, start, width)
+        pending.extend((g, t, start, width) for t in slots)
+        store_y(1, 5, False)
+        g, slots, start, width = products.pop(0)[1:]
+        second_stage(g, slots, start, width)
+        pending.extend((g, t, start, width) for t in slots)
+        for args in pending[:1]:
+            apply_gain(*args)
+        pending = pending[1:]
+        quantize_half(1, 0)
+        for args in pending[:2]:
+            apply_gain(*args)
+        pending = pending[2:]
+        g, slots, start, width = products.pop(0)[1:]
+        second_stage(g, slots, start, width)
+        pending.extend((g, t, start, width) for t in slots)
+        store_half(1, 0)
+        g, slots, start, width = products.pop(0)[1:]
+        second_stage(g, slots, start, width)
+        pending.extend((g, t, start, width) for t in slots)
+        for args in pending[:2]:
+            apply_gain(*args)
+        pending = pending[2:]
+        quantize_half(1, 1)
+        store_y(2, 0, False)
+        store_y(2, 1, False)
+        round_y(2, 0, False)
+        store_half(1, 1)
+        for args in pending[:4]:
+            apply_gain(*args)
+        pending = pending[4:]
+        g, slots, start, width = products.pop(0)[1:]
+        second_stage(g, slots, start, width)
+        pending.extend((g, t, start, width) for t in slots)
+        store_y(2, 2, False)
+        quantize_y(2, 0)
+        g, slots, start, width = products.pop(0)[1:]
+        second_stage(g, slots, start, width)
+        pending.extend((g, t, start, width) for t in slots)
+        store_y(2, 3, False)
+        round_y(2, 1, False)
+        store_codes(2, 0)
+        store_y(2, 4, True)
+        quantize_y(2, 1)
+        for args in pending[:4]:
+            apply_gain(*args)
+        pending = pending[4:]
+        store_y(2, 5, False)
+        g, slots, start, width = products.pop(0)[1:]
+        second_stage(g, slots, start, width)
+        pending.extend((g, t, start, width) for t in slots)
+        store_codes(2, 1)
+        store_y(3, 0, False)
+        round_y(2, 2, False)
+        g, slots, start, width = products.pop(0)[1:]
+        second_stage(g, slots, start, width)
+        pending.extend((g, t, start, width) for t in slots)
+        store_y(3, 1, False)
+        quantize_y(2, 2)
+        round_y(3, 0, False)
+        store_codes(2, 2)
+        for args in pending[:4]:
+            apply_gain(*args)
+        pending = pending[4:]
+        store_y(3, 2, False)
+        quantize_y(3, 0)
+        round_y(3, 1, False)
+        store_y(3, 3, False)
+        store_codes(3, 0)
+        quantize_y(3, 1)
+        round_y(3, 2, False)
+        store_y(3, 4, False)
+        store_codes(3, 1)
+        quantize_y(3, 2)
+        store_y(3, 5, False)
+        store_codes(3, 2)
 
         scale_words = out_2.bitcast(I32)
         for q in range(4):

@@ -19,14 +19,16 @@ P = 128
 PACK = 4
 K_PASS = P * PACK
 BANK = 512
-BANKS = 7
+RING_BANKS = 7
+LINE = 4
 TIME_PASSES = T // K_PASS
 GROUPS = F // K_PASS
-UNITS = GROUPS * PACK
-WIDE = 512
-NARROW = S - WIDE
+LAST = GROUPS - 1
+CHUNKS = F // P
 PIECE = 256
 PIECES = S // PIECE
+HALF = K_PASS // 2
+STAGE2_LAG = 3
 
 
 def tile_timestep_blend_conditioning_h3_kernel(
@@ -34,38 +36,41 @@ def tile_timestep_blend_conditioning_h3_kernel(
 ):
     nc = tc.nc
     with ExitStack() as ctx:
-        keep = ctx.enter_context(tc.tile_pool(name="keep", bufs=1))
+        sbuf = ctx.enter_context(tc.tile_pool(name="sbuf", bufs=1))
         psum = ctx.enter_context(tc.psum_pool(name="psum", bufs=1))
         ctx.enter_context(tc.manual_schedule())
 
-        uses = {}
+        turns = {}
 
-        def ring(pool, tag, depth, shape, dtype):
-            n = uses.get(tag, 0)
-            uses[tag] = n + 1
-            return pool.tile(shape, dtype, name=tag, tag="%s%d" % (tag, n % depth), align_bytes=64)
+        def next_tag(name, depth):
+            turn = turns.get(name, 0)
+            turns[name] = turn + 1
+            return "%s%d" % (name, turn % depth)
+
+        def ring(name, depth, shape, dtype):
+            return sbuf.tile(shape, dtype, name=name, tag=next_tag(name, depth), align_bytes=64)
 
         def next_bank():
-            n = uses.get("bank", 0)
-            uses["bank"] = n + 1
-            return psum.tile([P, BANK], F32, name="bank", tag="bank%d" % (n % BANKS))
+            return psum.tile([P, BANK], F32, name="bank", tag=next_tag("bank", RING_BANKS))
 
         def kept(name, shape, dtype):
-            return keep.tile(shape, dtype, name=name, tag=name, align_bytes=64)
+            return sbuf.tile(shape, dtype, name=name, tag=name, align_bytes=64)
 
         emb_rows = emb.rearrange("(h m t) k -> h m t k", m=P, t=PACK)
-        emb_raw = {}
-        w1_raw = {}
-        blend_raw = {}
+        emb_raw, w1_raw, blend_raw = {}, {}, {}
 
         def load_emb(h, pair):
             emb_raw[h, pair] = kept("emb_raw%d_%d" % (h, pair), [P, 2, D], BF16)
             nc.sync.dma_start(out=emb_raw[h, pair][:], in_=emb_rows[h, :, 2 * pair : 2 * pair + 2, :])
 
-        def load_w1(g, start=0, width=K_PASS):
-            w1_raw[g, start] = kept("w1_raw%d_%d" % (g, start), [P, PACK, width], BF16)
-            cols = w1[:, g * K_PASS + start : g * K_PASS + start + width]
-            nc.sync.dma_start(out=w1_raw[g, start][:], in_=cols.rearrange("(p j) c -> p j c", j=PACK))
+        def load_w1(g, halves):
+            width = len(halves) * HALF
+            first = g * K_PASS + halves[0] * HALF
+            raw = kept("w1_raw%d_%d" % (g, halves[0]), [P, PACK, width], BF16)
+            cols = w1[:, first : first + width]
+            nc.sync.dma_start(out=raw[:], in_=cols.rearrange("(p j) c -> p j c", j=PACK))
+            for i, half in enumerate(halves):
+                w1_raw[g, half] = raw[:, :, i * HALF : (i + 1) * HALF]
 
         def load_blend(piece):
             blend_raw[piece] = kept("blend_raw%d" % piece, [P, 2, T], BF16)
@@ -74,22 +79,22 @@ def tile_timestep_blend_conditioning_h3_kernel(
 
         load_emb(0, 0)
         load_emb(0, 1)
-        load_w1(0, 0, 2 * P)
+        load_w1(0, [0])
         load_emb(1, 0)
         load_emb(1, 1)
-        load_w1(0, 2 * P, K_PASS - 2 * P)
+        load_w1(0, [1])
         scale_rows = kept("scale_rows", [TIME_PASSES, K_PASS], BF16)
-        bias_sb = kept("bias_sb", [P, GROUPS, PACK], BF16)
-        gain_sb = kept("gain_sb", [P, GROUPS, PACK], BF16)
         nc.scalar.dma_start(out=scale_rows[:], in_=time_scale.rearrange("(h k) -> h k", h=TIME_PASSES))
-        load_w1(1)
+        load_w1(1, [0, 1])
         load_blend(0)
-        load_w1(2)
+        load_w1(2, [0, 1])
         load_blend(1)
         load_blend(2)
+        bias_sb = kept("bias_sb", [P, GROUPS, PACK], BF16)
+        gain_sb = kept("gain_sb", [P, GROUPS, PACK], BF16)
         nc.sync.dma_start(out=bias_sb[:], in_=bias.rearrange("(g p t) -> p g t", p=P, t=PACK))
         nc.sync.dma_start(out=gain_sb[:], in_=gain.rearrange("(g p t) -> p g t", p=P, t=PACK))
-        load_w1(3)
+        load_w1(3, [0, 1])
 
         ident = kept("ident", [P, P], F32)
         make_identity(nc, ident[:])
@@ -114,74 +119,68 @@ def tile_timestep_blend_conditioning_h3_kernel(
         def quantize(codes, scales, values):
             nc.vector.quantize_mx(out=codes.bitcast(FP8X4), scales=scales, in_=values)
 
-        def turn_rows(raw, h):
+        def gpsimd_copy(out, in_):
+            nc.gpsimd.tensor_scalar(out=out, in0=in_, scalar1=1.0, scalar2=1.0, op0=MULT, op1=MULT)
+
+        def interleave(values, rows, on_gpsimd):
+            if on_gpsimd:
+                gpsimd_copy(values.rearrange("p (c j) -> p c j", j=PACK), rows.rearrange("p j c -> p c j"))
+            else:
+                nc.vector.tensor_copy(
+                    out=values.rearrange("p (c i j) -> p c j i", i=LINE, j=PACK),
+                    in_=rows.rearrange("p j (c i) -> p c j i", i=LINE),
+                )
+
+        def staged():
+            return ring("staged", 2, [P, PIECE * PACK], BF16)
+
+        def turn_rows(raw, h, copy):
             words = raw[:].bitcast(F32)
             bank = next_bank()
             for a in range(2):
                 for u in range(2):
                     col = (2 * a + u) * P
-                    first = h * 2 * P + u
-                    nc.tensor.transpose(
-                        bank[:, col : col + P], words[:, a, first : (h + 1) * 2 * P : 2], ident[:]
-                    )
-            turned = ring(keep, "turned", 4, [P, 2 * P * PACK], BF16)
-            nc.scalar.copy(
+                    every_second = slice(h * 2 * P + u, (h + 1) * 2 * P, 2)
+                    nc.tensor.transpose(bank[:, col : col + P], words[:, a, every_second], ident[:])
+            turned = ring("turned", 4, [P, 2 * P * PACK], BF16)
+            copy(
                 out=turned[:].bitcast(F32).rearrange("p (a m u) -> p a m u", a=2, u=2),
                 in_=bank[:].rearrange("p (a u m) -> p a m u", a=2, u=2),
             )
             return turned
 
-        def quantize_emb(h, pair, turned):
+        def quantize_emb(h, pair):
             cols = slice((2 * h + pair) * 2 * P, (2 * h + pair + 1) * 2 * P)
-            quantize(emb_codes[:, cols], emb_scales[:, cols], turned[:])
+            quantize(emb_codes[:, cols], emb_scales[:, cols], emb_turned[h, pair][:])
 
-        def quantize_blend(piece, h, turned):
+        def quantize_blend(piece):
             cols = slice(piece * PIECE, (piece + 1) * PIECE)
-            quantize(blend_codes[:, h, cols], blend_scales[:, h, cols], turned[:])
+            for h in range(TIME_PASSES):
+                quantize(blend_codes[:, h, cols], blend_scales[:, h, cols], blend_turned[piece, h][:])
 
-        w1_grouped = {}
-        w1_mx = {}
-
-        def pool_copy(out, in_):
-            nc.gpsimd.tensor_scalar(out=out, in0=in_, scalar1=1.0, scalar2=1.0, op0=MULT, op1=MULT)
+        emb_turned, blend_turned, w1_values, w1_mx = {}, {}, {}, {}
 
         def interleave_w1(g, half, on_gpsimd):
-            base = max(b for (h, b) in w1_raw if h == g and b <= half * PIECE)
-            source = w1_raw[g, base][:, :, half * PIECE - base : (half + 1) * PIECE - base]
-            if g == 0:
-                values = ring(keep, "w1_first", 2, [P, PIECE * PACK], BF16)
-            else:
-                values = ring(keep, "staged", 2, [P, PIECE * PACK], BF16)
-            w1_grouped[g, half] = values
-            if on_gpsimd:
-                pool_copy(values[:].rearrange("p (c j) -> p c j", j=PACK), source.rearrange("p j c -> p c j"))
-            else:
-                nc.vector.tensor_copy(
-                    out=values[:].rearrange("p (c i j) -> p c j i", i=4, j=PACK),
-                    in_=source.rearrange("p j (c i) -> p c j i", i=4),
-                )
+            w1_values[g, half] = staged() if g > 0 else ring("w1_first", 2, [P, HALF * PACK], BF16)
+            interleave(w1_values[g, half][:], w1_raw[g, half], on_gpsimd)
 
         def quantize_w1(g, half):
             if half == 0:
-                w1_mx[g] = (
-                    ring(keep, "w1_codes", 2, [P, K_PASS], U32),
-                    ring(keep, "w1_scales", 2, [P, K_PASS], U8),
-                )
+                w1_mx[g] = ring("w1_codes", 2, [P, K_PASS], U32), ring("w1_scales", 2, [P, K_PASS], U8)
             codes, scales = w1_mx[g]
-            cols = slice(half * PIECE, (half + 1) * PIECE)
-            quantize(codes[:, cols], scales[:, cols], w1_grouped[g, half][:])
+            cols = slice(half * HALF, (half + 1) * HALF)
+            quantize(codes[:, cols], scales[:, cols], w1_values[g, half][:])
 
-        hidden = {}
-        z_bf16 = {}
-        z_mx = {}
+        hidden, z_values, z_mx = {}, {}, {}
 
-        def first_stage(n, passes=range(TIME_PASSES)):
-            g, c = divmod(n, PACK)
+        def first_stage(chunk):
+            g, c = divmod(chunk, PACK)
             codes, scales = w1_mx[g]
             feats = slice(c * P, (c + 1) * P)
-            if n % 2 == 0:
-                hidden[n // 2] = ring(keep, "hidden", 2, [P, TIME_PASSES, PACK, 2, P // PACK, PACK], F32)
-            for h in passes:
+            pair = chunk // 2
+            if pair not in hidden:
+                hidden[pair] = ring("hidden", 2, [P, TIME_PASSES, PACK, 2, P // PACK, PACK], F32)
+            for h in range(TIME_PASSES):
                 bank = next_bank()
                 for t in range(PACK):
                     cols = slice((h * PACK + t) * P, (h * PACK + t + 1) * P)
@@ -195,43 +194,42 @@ def tile_timestep_blend_conditioning_h3_kernel(
                         stop=True,
                     )
                 nc.scalar.activation(
-                    out=hidden[n // 2][:, h, :, n % 2],
+                    out=hidden[pair][:, h, :, chunk % 2],
                     in_=bank[:].rearrange("p (t m s) -> p s m t", t=PACK, s=PACK),
                     func=SILU,
                 )
 
         def scale_hidden(pair):
-            g, c = divmod(pair, 2)
-            if c == 0:
-                z_bf16[g] = ring(keep, "z_bf16", 2, [P, PACK, TIME_PASSES, P, PACK], BF16)
-            half = P // 2
+            g, half = divmod(pair, 2)
+            if half == 0:
+                z_values[g] = ring("z_values", 2, [P, PACK, TIME_PASSES, P, PACK], BF16)
+            part = z_values[g][:, :, :, half * P // 2 : (half + 1) * P // 2, :]
             nc.vector.tensor_tensor(
-                out=z_bf16[g][:, :, :, c * half : (c + 1) * half, :].rearrange("p s h m t -> p h s (m t)"),
+                out=part.rearrange("p s h m t -> p h s (m t)"),
                 in0=hidden[pair][:].rearrange("p h s c m t -> p h (s c m) t"),
                 in1=scale_view.unsqueeze(2).to_broadcast([P, TIME_PASSES, 2 * P, PACK]),
                 op=MULT,
             )
 
-        def quantize_z(g, half):
-            codes = ring(keep, "z_codes", 4, [P, 2, TIME_PASSES * P], U32)
-            scales = ring(keep, "z_scales", 4, [P, 2, TIME_PASSES * P], U8)
-            quantize(
-                codes[:].rearrange("p s w -> p (s w)"),
-                scales[:].rearrange("p s w -> p (s w)"),
-                z_bf16[g][:, 2 * half : 2 * half + 2].rearrange("p s h m t -> p (s h m t)"),
-            )
-            for i in range(2):
-                z_mx[g * PACK + 2 * half + i] = codes[:, i, :], scales[:, i, :]
+        def quantize_z(g):
+            for first in (0, 2):
+                codes = ring("z_codes", 4, [P, 2, TIME_PASSES * P], U32)
+                scales = ring("z_scales", 4, [P, 2, TIME_PASSES * P], U8)
+                quantize(
+                    codes[:].rearrange("p s w -> p (s w)"),
+                    scales[:].rearrange("p s w -> p (s w)"),
+                    z_values[g][:, first : first + 2].rearrange("p s h m t -> p (s h m t)"),
+                )
+                for i in range(2):
+                    z_mx[g, first + i] = codes[:, i, :], scales[:, i, :]
 
-        silu_out = {}
-        y_turned = {}
-        complete = []
+        silu_out, y_turned = {}, {}
 
         def second_stage(g, slots, start, width):
             bank = next_bank()
             rows = slice(start, start + width)
             for i, t in enumerate(slots):
-                codes, scales = z_mx[g * PACK + t]
+                codes, scales = z_mx[g, t]
                 for h in range(TIME_PASSES):
                     nc.tensor.matmul_mx(
                         out=bank[:, i * width : (i + 1) * width],
@@ -244,285 +242,163 @@ def tile_timestep_blend_conditioning_h3_kernel(
                     )
             for i, t in enumerate(slots):
                 if (g, t) not in silu_out:
-                    silu_out[g, t] = ring(keep, "silu_out", 6, [P, S], F32)
+                    silu_out[g, t] = ring("silu_out", 6, [P, S], F32)
                 nc.scalar.activation(
                     out=silu_out[g, t][:, rows],
                     in_=bank[:, i * width : (i + 1) * width],
                     func=SILU,
                     bias=bias_sb[:, g, t : t + 1],
                 )
+            return [(g, t, start, width) for t in slots]
 
-        def apply_gain(g, t, start, width):
-            if t == PACK - 1 and g >= 2:
-                complete.extend((g, piece) for piece in range(start // PIECE, (start + width) // PIECE))
-            if g not in y_turned:
-                y_turned[g] = ring(keep, "y_turned", 3, [P, PACK, S], F32)
-            nc.vector.tensor_scalar(
-                out=y_turned[g][:, t, start : start + width],
-                in0=silu_out[g, t][:, start : start + width],
-                scalar1=gain_sb[:, g, t : t + 1],
-                scalar2=None,
-                op0=MULT,
-            )
+        def apply_gains(due):
+            for g, t, start, width in due:
+                if g not in y_turned:
+                    y_turned[g] = ring("y_turned", 3, [P, PACK, S], F32)
+                nc.vector.tensor_scalar(
+                    out=y_turned[g][:, t, start : start + width],
+                    in0=silu_out[g, t][:, start : start + width],
+                    scalar1=gain_sb[:, g, t : t + 1],
+                    scalar2=None,
+                    op0=MULT,
+                )
 
-        def y_window(g, row, count):
-            return y_turned[g][:, :, row : row + count]
-
-        HALF = S // 2
-        y_half = {}
-        half_codes = {}
-
-        def round_half(g, half):
-            y_half[g, half] = ring(keep, "staged", 2, [P, HALF * PACK], BF16)
-            pool_copy(
-                y_half[g, half][:].rearrange("p (m t) -> p m t", t=PACK),
-                y_window(g, half * HALF, HALF).rearrange("p t m -> p m t"),
-            )
-
-        def quantize_half(g, half):
-            codes = ring(keep, "y_half_codes", 2, [P, HALF], U32)
-            for start, width in ((0, PIECE), (PIECE, HALF - PIECE)):
-                cols = slice(half * HALF + start, half * HALF + start + width)
-                values = y_half[g, half][:, start * PACK : (start + width) * PACK]
-                quantize(codes[:, start : start + width], y_scales[PACK * g :, cols], values)
-            half_codes[g, half] = codes
-
-        def store_half(g, half):
-            words = out_1[g].rearrange("p m t -> p (m t)").bitcast(I32)
-            nc.sync.dma_start(
-                out=words[:, half * HALF : (half + 1) * HALF], in_=half_codes[g, half][:].bitcast(I32)
-            )
-
-        def store_y(g, a, late_copy):
-            source = y_window(g, a * P, P)
+        def store_tile(g, a, copy=nc.scalar.copy):
             bank = next_bank()
             for t in range(PACK):
-                nc.tensor.transpose(bank[:, t * P : (t + 1) * P], source[:, t, :], ident[:])
+                source = y_turned[g][:, t, a * P : (a + 1) * P]
+                nc.tensor.transpose(bank[:, t * P : (t + 1) * P], source, ident[:])
+            rows = ring("y_rows", 6, [P, K_PASS], F32)
+            copy(
+                out=rows[:].rearrange("s (p t) -> s p t", t=PACK),
+                in_=bank[:].rearrange("s (t p) -> s p t", t=PACK),
+            )
+            nc.sync.dma_start(out=out_0[a * P : (a + 1) * P, g * K_PASS : (g + 1) * K_PASS], in_=rows[:])
 
-            def finish(copy):
-                rows = ring(keep, "y_rows", 6, [P, K_PASS], F32)
-                copy(
-                    out=rows[:].rearrange("s (p t) -> s p t", t=PACK),
-                    in_=bank[:].rearrange("s (t p) -> s p t", t=PACK),
-                )
-                nc.sync.dma_start(
-                    out=out_0[a * P : (a + 1) * P, g * K_PASS : (g + 1) * K_PASS], in_=rows[:]
-                )
+        y_values, y_codes = {}, {}
 
-            if late_copy:
-                finish(nc.vector.tensor_copy)
-            else:
-                finish(nc.scalar.copy)
+        def round_y(n, on_gpsimd):
+            g, piece = divmod(n, PIECES)
+            y_values[n] = staged() if on_gpsimd else ring("y_values", 3, [P, PIECE * PACK], BF16)
+            interleave(y_values[n][:], y_turned[g][:, :, piece * PIECE : (piece + 1) * PIECE], on_gpsimd)
 
-        late = []
-        y_bf16 = {}
-        y_codes = {}
+        def quantize_y(n):
+            g, piece = divmod(n, PIECES)
+            y_codes[n] = ring("y_codes", 6, [P, PIECE], U32)
+            scales = y_scales[PACK * g :, piece * PIECE : (piece + 1) * PIECE]
+            quantize(y_codes[n][:], scales, y_values[n][:])
 
-        def round_y(g, piece, on_gpsimd):
-            source = y_window(g, piece * PIECE, PIECE)
-            if on_gpsimd:
-                y_bf16[g, piece] = ring(keep, "y_bf16_g", 1, [P, PIECE * PACK], BF16)
-                nc.gpsimd.tensor_scalar(
-                    out=y_bf16[g, piece][:].rearrange("p (m t) -> p m t", t=PACK),
-                    in0=source.rearrange("p t m -> p m t"),
-                    scalar1=1.0,
-                    scalar2=1.0,
-                    op0=MULT,
-                    op1=MULT,
-                )
-                return
-            y_bf16[g, piece] = ring(keep, "y_bf16", 2, [P, PIECE * PACK], BF16)
-            nc.vector.tensor_copy(
-                out=y_bf16[g, piece][:].rearrange("p (c i t) -> p c t i", i=4, t=PACK),
-                in_=source.rearrange("p t (c i) -> p c t i", i=4),
+        def store_codes(n):
+            g, piece = divmod(n, PIECES)
+            words = out_1[g].rearrange("p m t -> p (m t)").bitcast(I32)
+            nc.sync.dma_start(
+                out=words[:, piece * PIECE : (piece + 1) * PIECE], in_=y_codes[n][:].bitcast(I32)
             )
 
-        def quantize_y(g, piece):
-            cols = slice(piece * PIECE, (piece + 1) * PIECE)
-            codes = ring(keep, "y_codes", 6, [P, PIECE], U32)
-            quantize(codes[:], y_scales[PACK * g :, cols], y_bf16[g, piece][:])
-            y_codes[g, piece] = codes
-
-        def store_codes(g, piece):
-            cols = slice(piece * PIECE, (piece + 1) * PIECE)
-            words = out_1[g].rearrange("p m t -> p (m t)").bitcast(I32)
-            nc.sync.dma_start(out=words[:, cols], in_=y_codes[g, piece][:].bitcast(I32))
-
-        on_scalar, on_vector = nc.scalar.copy, nc.vector.tensor_copy
-        turned = [turn_rows(emb_raw[h, pair], 0) for h in range(TIME_PASSES) for pair in range(2)]
+        for h in range(TIME_PASSES):
+            for pair in range(2):
+                emb_turned[h, pair] = turn_rows(emb_raw[h, pair], 0, nc.scalar.copy)
         for t in range(PACK):
-            nc.tensor.transpose(scale_bank[:, t * P : (t + 1) * P], scale_sorted[:, t * P : (t + 1) * P], ident[:])
-        quantize_emb(0, 0, turned[0])
+            cols = slice(t * P, (t + 1) * P)
+            nc.tensor.transpose(scale_bank[:, cols], scale_sorted[:, cols], ident[:])
+        quantize_emb(0, 0)
         interleave_w1(0, 0, False)
-        quantize_emb(0, 1, turned[1])
+        quantize_emb(0, 1)
         quantize_w1(0, 0)
-        quantize_emb(1, 0, turned[2])
-        quantize_emb(1, 1, turned[3])
+        quantize_emb(1, 0)
+        quantize_emb(1, 1)
         interleave_w1(0, 1, False)
         interleave_w1(1, 0, False)
         quantize_w1(0, 1)
         interleave_w1(1, 1, False)
 
-        last = GROUPS - 1
-        rounded, quantized, stored = [], [], []
+        wide = [([t], 0, BANK) for t in range(PACK)] + [(s, BANK, S - BANK) for s in ([0, 1], [2, 3])]
+        narrow = [(s, piece * PIECE, PIECE) for piece in range(PIECES) for s in ([0, 1], [2, 3])]
+        products = [(g,) + bank for g in range(GROUPS) for bank in (wide if g < LAST else narrow)]
 
-        def advance_planes(on_gpsimd):
-            if len(stored) < len(quantized):
-                stored.append(quantized[len(stored)])
-                store_codes(*stored[-1])
-            if len(quantized) < len(rounded):
-                quantized.append(rounded[len(quantized)])
-                quantize_y(*quantized[-1])
-            if len(rounded) < len(complete):
-                rounded.append(complete[len(rounded)])
-                round_y(*rounded[-1], on_gpsimd)
+        gpsimd_pieces = [0, 1, 2, 4]
+        w1_halves = [(g, half) for g in range(1, GROUPS) for half in range(2)]
 
-        wide = [([0], 0, WIDE), ([1], 0, WIDE), ([2], 0, WIDE), ([3], 0, WIDE), ([0, 1], WIDE, NARROW), ([2, 3], WIDE, NARROW)]
-        narrow = [(slots, piece * PIECE, PIECE) for piece in range(PIECES) for slots in ([0, 1], [2, 3])]
-        products = [(PACK * g + PACK + 2, g) + b for g in range(GROUPS) for b in (wide if g < last else narrow)]
-        pattern = ["sts", "tst", "sts", "tst"]
-        pending, tiles = [], []
-        done = 0
-        step = 0
-        while step < UNITS:
-            k = step % PACK
-            if step < UNITS:
-                first_stage(step)
-            if k == 0 and 0 < step <= UNITS:
-                quantize_z(step // PACK - 1, 0)
-                quantize_z(step // PACK - 1, 1)
-            for args in pending:
-                apply_gain(*args)
-                if args[1] == PACK - 1:
-                    for a in range(args[2] // P, (args[2] + args[3]) // P):
-                        tiles.append((step + 1, args[0], a))
-            pending = []
-            if 2 <= step <= PIECES + 1:
-                for h, values in enumerate(blend_turned):
-                    quantize_blend(step - 2, h, values)
-            if step % 2 == 1 and step < UNITS:
-                j = step // 2
-                if j < 6:
-                    quantize_w1(1 + j // 2, j % 2)
+        due, tiles, tiles_next = [], [], []
+        for step in range(CHUNKS):
+            first_stage(step)
+            if step % PACK == 0 and step > 0:
+                quantize_z(step // PACK - 1)
+            apply_gains(due)
+            tiles.extend(tiles_next)
+            tiles_next = [
+                (g, a)
+                for g, t, start, width in due
+                if t == PACK - 1
+                for a in range(start // P, (start + width) // P)
+            ]
+            due = []
+            if 2 <= step < 2 + PIECES:
+                quantize_blend(step - 2)
+            if step % 2 == 1:
+                pair = step // 2
+                if pair < len(w1_halves):
+                    quantize_w1(*w1_halves[pair])
                 else:
-                    quantize_half(0, j - 6)
-                if j < 4:
-                    interleave_w1(2 + j // 2, j % 2, True)
+                    quantize_y(gpsimd_pieces[pair - len(w1_halves)])
+                if pair + 2 < len(w1_halves):
+                    interleave_w1(*w1_halves[pair + 2], True)
                 else:
-                    round_half((j - 4) // 2, j % 2)
-                scale_hidden(j)
-            if step in (14, 16):
-                store_half(0, (step - 14) // 2)
-            if step in (16, 17):
-                quantize_half(1, step - 16)
-            if step in (17, 18):
-                store_half(1, step - 17)
-            if step >= UNITS:
-                advance_planes(False)
-            if step > UNITS:
-                advance_planes(False)
-            if 1 <= step <= PIECES:
-                blend_turned = [turn_rows(blend_raw[step - 1], h) for h in range(TIME_PASSES)]
-            for i, item in enumerate(pattern[k] if step < UNITS else "tstst"):
-                if item == "s" and products and products[0][0] <= step:
-                    g, slots, start, width = products.pop(0)[1:]
-                    second_stage(g, slots, start, width)
-                    pending.extend((g, t, start, width) for t in slots)
-                if item == "t" and tiles and tiles[0][0] <= step:
-                    store_y(*tiles.pop(0)[1:], (step % 2 == 1 and i == 2) if step < UNITS else (False))
-                    done = done + 1
-            step = step + 1
-        quantize_z(last, 0)
-        quantize_z(last, 1)
-        for args in pending[:1]:
-            apply_gain(*args)
-        pending = pending[1:]
-        store_y(1, 3, False)
-        store_half(0, 1)
-        g, slots, start, width = products.pop(0)[1:]
-        second_stage(g, slots, start, width)
-        pending.extend((g, t, start, width) for t in slots)
-        store_y(1, 4, False)
-        g, slots, start, width = products.pop(0)[1:]
-        second_stage(g, slots, start, width)
-        pending.extend((g, t, start, width) for t in slots)
-        store_y(1, 5, False)
-        g, slots, start, width = products.pop(0)[1:]
-        second_stage(g, slots, start, width)
-        pending.extend((g, t, start, width) for t in slots)
-        for args in pending[:1]:
-            apply_gain(*args)
-        pending = pending[1:]
-        quantize_half(1, 0)
-        for args in pending[:2]:
-            apply_gain(*args)
-        pending = pending[2:]
-        g, slots, start, width = products.pop(0)[1:]
-        second_stage(g, slots, start, width)
-        pending.extend((g, t, start, width) for t in slots)
-        store_half(1, 0)
-        g, slots, start, width = products.pop(0)[1:]
-        second_stage(g, slots, start, width)
-        pending.extend((g, t, start, width) for t in slots)
-        for args in pending[:2]:
-            apply_gain(*args)
-        pending = pending[2:]
-        quantize_half(1, 1)
-        store_y(2, 0, False)
-        store_y(2, 1, False)
-        round_y(2, 0, False)
-        store_half(1, 1)
-        for args in pending[:4]:
-            apply_gain(*args)
-        pending = pending[4:]
-        g, slots, start, width = products.pop(0)[1:]
-        second_stage(g, slots, start, width)
-        pending.extend((g, t, start, width) for t in slots)
-        store_y(2, 2, False)
-        quantize_y(2, 0)
-        g, slots, start, width = products.pop(0)[1:]
-        second_stage(g, slots, start, width)
-        pending.extend((g, t, start, width) for t in slots)
-        store_y(2, 3, False)
-        round_y(2, 1, False)
-        store_codes(2, 0)
-        store_y(2, 4, True)
-        quantize_y(2, 1)
-        for args in pending[:4]:
-            apply_gain(*args)
-        pending = pending[4:]
-        store_y(2, 5, False)
-        g, slots, start, width = products.pop(0)[1:]
-        second_stage(g, slots, start, width)
-        pending.extend((g, t, start, width) for t in slots)
-        store_codes(2, 1)
-        store_y(3, 0, False)
-        round_y(2, 2, False)
-        g, slots, start, width = products.pop(0)[1:]
-        second_stage(g, slots, start, width)
-        pending.extend((g, t, start, width) for t in slots)
-        store_y(3, 1, False)
-        quantize_y(2, 2)
-        round_y(3, 0, False)
-        store_codes(2, 2)
-        for args in pending[:4]:
-            apply_gain(*args)
-        pending = pending[4:]
-        store_y(3, 2, False)
-        quantize_y(3, 0)
-        round_y(3, 1, False)
-        store_y(3, 3, False)
-        store_codes(3, 0)
-        quantize_y(3, 1)
-        round_y(3, 2, False)
-        store_y(3, 4, False)
-        store_codes(3, 1)
-        quantize_y(3, 2)
-        store_y(3, 5, False)
-        store_codes(3, 2)
+                    round_y(gpsimd_pieces[pair + 2 - len(w1_halves)], True)
+                scale_hidden(pair)
+            if step == CHUNKS - 2:
+                store_codes(0)
+                round_y(3, False)
+            if 1 <= step < 1 + PIECES:
+                for h in range(TIME_PASSES):
+                    copy = nc.vector.tensor_copy if step == 1 and h == 1 else nc.scalar.copy
+                    blend_turned[step - 1, h] = turn_rows(blend_raw[step - 1], h, copy)
+            for place in range(3):
+                if (step + place) % 2 == 0:
+                    if step >= PACK * products[0][0] + PACK - 1 + STAGE2_LAG:
+                        due.extend(second_stage(*products.pop(0)))
+                elif tiles:
+                    on_vector = step % 2 == 1 and place == 2
+                    store_tile(*tiles.pop(0), nc.vector.tensor_copy if on_vector else nc.scalar.copy)
+
+        quantize_z(LAST)
+        apply_gains(due)
+        last_gains = []
+        for tile in tiles:
+            store_tile(*tile)
+            last_gains.append(second_stage(*products.pop(0)))
+        store_codes(1)
+        apply_gains(last_gains[0])
+        quantize_y(2)
+        apply_gains(last_gains[1])
+        quantize_y(3)
+        apply_gains(last_gains[2])
+        store_codes(2)
+
+        for piece in range(PIECES):
+            due = second_stage(*products.pop(0)) + second_stage(*products.pop(0))
+            n = gpsimd_pieces[-1] + 2 * piece
+            round_y(n + 1, False)
+            quantize_y(n)
+            store_tile(LAST - 1, 2 * piece)
+            store_tile(LAST - 1, 2 * piece + 1)
+            store_codes(n - 1)
+            store_codes(n)
+            apply_gains(due)
+            round_y(n + 2, False)
+            quantize_y(n + 1)
+
+        final = GROUPS * PIECES - 1
+        round_y(final, False)
+        quantize_y(final - 1)
+        quantize_y(final)
+        for piece in range(PIECES):
+            store_tile(LAST, 2 * piece)
+            store_tile(LAST, 2 * piece + 1)
+            store_codes(LAST * PIECES + piece)
 
         scale_words = out_2.bitcast(I32)
-        for q in range(4):
+        for q in range(P // 32):
             nc.sync.dma_start(
                 out=scale_words[:, PACK * q : PACK * q + PACK, :],
                 in_=y_scales[32 * q : 32 * q + PACK * GROUPS, :].bitcast(I32),

from contextlib import ExitStack

import concourse.mybir as mybir
from concourse.masks import make_identity

T, D, F, S = 1024, 512, 2048, 768
FLOPS = 2 * T * D * F + 2 * S * T * F

F32 = mybir.dt.float32
BF16 = mybir.dt.bfloat16
I32 = mybir.dt.int32
U32 = mybir.dt.uint32
U8 = mybir.dt.uint8
FP8X4 = mybir.dt.float8_e4m3fn_x4
SILU = mybir.ActivationFunctionType.Silu
MULT = mybir.AluOpType.mult

P = 128
PACK = 4
K_PASS = P * PACK
BANK = 512
RING_BANKS = 7
LINE = 4
TIME_PASSES = T // K_PASS
GROUPS = F // K_PASS
LAST = GROUPS - 1
CHUNKS = F // P
PIECE = 256
PIECES = S // PIECE
HALF = K_PASS // 2
STAGE2_LAG = 3


def tile_timestep_blend_conditioning_h3_kernel(
    tc, emb, w1, time_scale, blend, bias, gain, out_0, out_1, out_2
):
    nc = tc.nc
    with ExitStack() as ctx:
        sbuf = ctx.enter_context(tc.tile_pool(name="sbuf", bufs=1))
        psum = ctx.enter_context(tc.psum_pool(name="psum", bufs=1))
        ctx.enter_context(tc.manual_schedule())

        turns = {}

        def next_tag(name, depth):
            turn = turns.get(name, 0)
            turns[name] = turn + 1
            return "%s%d" % (name, turn % depth)

        def ring(name, depth, shape, dtype):
            return sbuf.tile(shape, dtype, name=name, tag=next_tag(name, depth), align_bytes=64)

        def next_bank():
            return psum.tile([P, BANK], F32, name="bank", tag=next_tag("bank", RING_BANKS))

        def kept(name, shape, dtype):
            return sbuf.tile(shape, dtype, name=name, tag=name, align_bytes=64)

        emb_rows = emb.rearrange("(h m t) k -> h m t k", m=P, t=PACK)
        emb_raw, w1_raw, blend_raw = {}, {}, {}

        def load_emb(h, pair):
            emb_raw[h, pair] = kept("emb_raw%d_%d" % (h, pair), [P, 2, D], BF16)
            nc.sync.dma_start(out=emb_raw[h, pair][:], in_=emb_rows[h, :, 2 * pair : 2 * pair + 2, :])

        def load_w1(g, halves):
            width = len(halves) * HALF
            first = g * K_PASS + halves[0] * HALF
            raw = kept("w1_raw%d_%d" % (g, halves[0]), [P, PACK, width], BF16)
            cols = w1[:, first : first + width]
            nc.sync.dma_start(out=raw[:], in_=cols.rearrange("(p j) c -> p j c", j=PACK))
            for i, half in enumerate(halves):
                w1_raw[g, half] = raw[:, :, i * HALF : (i + 1) * HALF]

        def load_blend(piece):
            blend_raw[piece] = kept("blend_raw%d" % piece, [P, 2, T], BF16)
            rows = blend[piece * PIECE : (piece + 1) * PIECE, :]
            nc.sync.dma_start(out=blend_raw[piece][:], in_=rows.rearrange("(a m) k -> m a k", m=P))

        load_emb(0, 0)
        load_emb(0, 1)
        load_w1(0, [0])
        load_emb(1, 0)
        load_emb(1, 1)
        load_w1(0, [1])
        scale_rows = kept("scale_rows", [TIME_PASSES, K_PASS], BF16)
        nc.scalar.dma_start(out=scale_rows[:], in_=time_scale.rearrange("(h k) -> h k", h=TIME_PASSES))
        load_w1(1, [0, 1])
        load_blend(0)
        load_w1(2, [0, 1])
        load_blend(1)
        load_blend(2)
        bias_sb = kept("bias_sb", [P, GROUPS, PACK], BF16)
        gain_sb = kept("gain_sb", [P, GROUPS, PACK], BF16)
        nc.sync.dma_start(out=bias_sb[:], in_=bias.rearrange("(g p t) -> p g t", p=P, t=PACK))
        nc.sync.dma_start(out=gain_sb[:], in_=gain.rearrange("(g p t) -> p g t", p=P, t=PACK))
        load_w1(3, [0, 1])

        ident = kept("ident", [P, P], F32)
        make_identity(nc, ident[:])
        warm = kept("warm", [P, 1], F32)
        nc.scalar.activation(out=warm[:], in_=ident[:, 0:1], func=SILU)

        scale_sorted = kept("scale_sorted", [P, K_PASS], F32)
        nc.vector.memset(scale_sorted[:], 0.0)
        nc.vector.tensor_copy(
            out=scale_sorted[0:TIME_PASSES, :].rearrange("h (t p) -> h t p", t=PACK),
            in_=scale_rows[:].rearrange("h (p t) -> h t p", t=PACK),
        )
        scale_bank = psum.tile([P, BANK], F32, name="scale_bank", tag="scale_bank")
        scale_view = scale_bank[:].rearrange("p (t h) -> p h t", t=PACK)[:, 0:TIME_PASSES, :]

        emb_codes = kept("emb_codes", [P, T], U32)
        emb_scales = kept("emb_scales", [P, T], U8)
        blend_codes = kept("blend_codes", [P, TIME_PASSES, S], U32)
        blend_scales = kept("blend_scales", [P, TIME_PASSES, S], U8)
        y_scales = kept("y_scales", [P, S], U8)

        def quantize(codes, scales, values):
            nc.vector.quantize_mx(out=codes.bitcast(FP8X4), scales=scales, in_=values)

        def gpsimd_copy(out, in_):
            nc.gpsimd.tensor_scalar(out=out, in0=in_, scalar1=1.0, scalar2=1.0, op0=MULT, op1=MULT)

        def interleave(values, rows, on_gpsimd):
            if on_gpsimd:
                gpsimd_copy(values.rearrange("p (c j) -> p c j", j=PACK), rows.rearrange("p j c -> p c j"))
            else:
                nc.vector.tensor_copy(
                    out=values.rearrange("p (c i j) -> p c j i", i=LINE, j=PACK),
                    in_=rows.rearrange("p j (c i) -> p c j i", i=LINE),
                )

        def staged():
            return ring("staged", 2, [P, PIECE * PACK], BF16)

        def turn_rows(raw, h, copy):
            words = raw[:].bitcast(F32)
            bank = next_bank()
            for a in range(2):
                for u in range(2):
                    col = (2 * a + u) * P
                    every_second = slice(h * 2 * P + u, (h + 1) * 2 * P, 2)
                    nc.tensor.transpose(bank[:, col : col + P], words[:, a, every_second], ident[:])
            turned = ring("turned", 4, [P, 2 * P * PACK], BF16)
            copy(
                out=turned[:].bitcast(F32).rearrange("p (a m u) -> p a m u", a=2, u=2),
                in_=bank[:].rearrange("p (a u m) -> p a m u", a=2, u=2),
            )
            return turned

        def quantize_emb(h, pair):
            cols = slice((2 * h + pair) * 2 * P, (2 * h + pair + 1) * 2 * P)
            quantize(emb_codes[:, cols], emb_scales[:, cols], emb_turned[h, pair][:])

        def quantize_blend(piece):
            cols = slice(piece * PIECE, (piece + 1) * PIECE)
            for h in range(TIME_PASSES):
                quantize(blend_codes[:, h, cols], blend_scales[:, h, cols], blend_turned[piece, h][:])

        emb_turned, blend_turned, w1_values, w1_mx = {}, {}, {}, {}

        def interleave_w1(g, half, on_gpsimd):
            w1_values[g, half] = staged() if g > 0 else ring("w1_first", 2, [P, HALF * PACK], BF16)
            interleave(w1_values[g, half][:], w1_raw[g, half], on_gpsimd)

        def quantize_w1(g, half):
            if half == 0:
                w1_mx[g] = ring("w1_codes", 2, [P, K_PASS], U32), ring("w1_scales", 2, [P, K_PASS], U8)
            codes, scales = w1_mx[g]
            cols = slice(half * HALF, (half + 1) * HALF)
            quantize(codes[:, cols], scales[:, cols], w1_values[g, half][:])

        hidden, z_values, z_mx = {}, {}, {}

        def first_stage(chunk):
            g, c = divmod(chunk, PACK)
            codes, scales = w1_mx[g]
            feats = slice(c * P, (c + 1) * P)
            pair = chunk // 2
            if pair not in hidden:
                hidden[pair] = ring("hidden", 2, [P, TIME_PASSES, PACK, 2, P // PACK, PACK], F32)
            for h in range(TIME_PASSES):
                bank = next_bank()
                for t in range(PACK):
                    cols = slice((h * PACK + t) * P, (h * PACK + t + 1) * P)
                    nc.tensor.matmul_mx(
                        out=bank[:, t * P : (t + 1) * P],
                        lhsT=emb_codes[:, cols].bitcast(FP8X4),
                        lhsT_scale=emb_scales[:, cols],
                        rhs=codes[:, feats].bitcast(FP8X4),
                        rhs_scale=scales[:, feats],
                        start=True,
                        stop=True,
                    )
                nc.scalar.activation(
                    out=hidden[pair][:, h, :, chunk % 2],
                    in_=bank[:].rearrange("p (t m s) -> p s m t", t=PACK, s=PACK),
                    func=SILU,
                )

        def scale_hidden(pair):
            g, half = divmod(pair, 2)
            if half == 0:
                z_values[g] = ring("z_values", 2, [P, PACK, TIME_PASSES, P, PACK], BF16)
            part = z_values[g][:, :, :, half * P // 2 : (half + 1) * P // 2, :]
            nc.vector.tensor_tensor(
                out=part.rearrange("p s h m t -> p h s (m t)"),
                in0=hidden[pair][:].rearrange("p h s c m t -> p h (s c m) t"),
                in1=scale_view.unsqueeze(2).to_broadcast([P, TIME_PASSES, 2 * P, PACK]),
                op=MULT,
            )

        def quantize_z(g):
            for first in (0, 2):
                codes = ring("z_codes", 4, [P, 2, TIME_PASSES * P], U32)
                scales = ring("z_scales", 4, [P, 2, TIME_PASSES * P], U8)
                quantize(
                    codes[:].rearrange("p s w -> p (s w)"),
                    scales[:].rearrange("p s w -> p (s w)"),
                    z_values[g][:, first : first + 2].rearrange("p s h m t -> p (s h m t)"),
                )
                for i in range(2):
                    z_mx[g, first + i] = codes[:, i, :], scales[:, i, :]

        silu_out, y_turned = {}, {}

        def second_stage(g, slots, start, width):
            bank = next_bank()
            rows = slice(start, start + width)
            for i, t in enumerate(slots):
                codes, scales = z_mx[g, t]
                for h in range(TIME_PASSES):
                    nc.tensor.matmul_mx(
                        out=bank[:, i * width : (i + 1) * width],
                        lhsT=codes[:, h * P : (h + 1) * P].bitcast(FP8X4),
                        lhsT_scale=scales[:, h * P : (h + 1) * P],
                        rhs=blend_codes[:, h, rows].bitcast(FP8X4),
                        rhs_scale=blend_scales[:, h, rows],
                        start=(h == 0),
                        stop=(h == TIME_PASSES - 1),
                    )
            for i, t in enumerate(slots):
                if (g, t) not in silu_out:
                    silu_out[g, t] = ring("silu_out", 6, [P, S], F32)
                nc.scalar.activation(
                    out=silu_out[g, t][:, rows],
                    in_=bank[:, i * width : (i + 1) * width],
                    func=SILU,
                    bias=bias_sb[:, g, t : t + 1],
                )
            return [(g, t, start, width) for t in slots]

        def apply_gains(due):
            for g, t, start, width in due:
                if g not in y_turned:
                    y_turned[g] = ring("y_turned", 3, [P, PACK, S], F32)
                nc.vector.tensor_scalar(
                    out=y_turned[g][:, t, start : start + width],
                    in0=silu_out[g, t][:, start : start + width],
                    scalar1=gain_sb[:, g, t : t + 1],
                    scalar2=None,
                    op0=MULT,
                )

        def store_tile(g, a, copy=nc.scalar.copy):
            bank = next_bank()
            for t in range(PACK):
                source = y_turned[g][:, t, a * P : (a + 1) * P]
                nc.tensor.transpose(bank[:, t * P : (t + 1) * P], source, ident[:])
            rows = ring("y_rows", 6, [P, K_PASS], F32)
            copy(
                out=rows[:].rearrange("s (p t) -> s p t", t=PACK),
                in_=bank[:].rearrange("s (t p) -> s p t", t=PACK),
            )
            nc.sync.dma_start(out=out_0[a * P : (a + 1) * P, g * K_PASS : (g + 1) * K_PASS], in_=rows[:])

        y_values, y_codes = {}, {}

        def round_y(n, on_gpsimd):
            g, piece = divmod(n, PIECES)
            y_values[n] = staged() if on_gpsimd else ring("y_values", 3, [P, PIECE * PACK], BF16)
            interleave(y_values[n][:], y_turned[g][:, :, piece * PIECE : (piece + 1) * PIECE], on_gpsimd)

        def quantize_y(n):
            g, piece = divmod(n, PIECES)
            y_codes[n] = ring("y_codes", 6, [P, PIECE], U32)
            scales = y_scales[PACK * g :, piece * PIECE : (piece + 1) * PIECE]
            quantize(y_codes[n][:], scales, y_values[n][:])

        def store_codes(n):
            g, piece = divmod(n, PIECES)
            words = out_1[g].rearrange("p m t -> p (m t)").bitcast(I32)
            nc.sync.dma_start(
                out=words[:, piece * PIECE : (piece + 1) * PIECE], in_=y_codes[n][:].bitcast(I32)
            )

        for h in range(TIME_PASSES):
            for pair in range(2):
                emb_turned[h, pair] = turn_rows(emb_raw[h, pair], 0, nc.scalar.copy)
        for t in range(PACK):
            cols = slice(t * P, (t + 1) * P)
            nc.tensor.transpose(scale_bank[:, cols], scale_sorted[:, cols], ident[:])
        quantize_emb(0, 0)
        interleave_w1(0, 0, False)
        quantize_emb(0, 1)
        quantize_w1(0, 0)
        quantize_emb(1, 0)
        quantize_emb(1, 1)
        interleave_w1(0, 1, False)
        interleave_w1(1, 0, False)
        quantize_w1(0, 1)
        interleave_w1(1, 1, False)

        wide = [([t], 0, BANK) for t in range(PACK)] + [(s, BANK, S - BANK) for s in ([0, 1], [2, 3])]
        narrow = [(s, piece * PIECE, PIECE) for piece in range(PIECES) for s in ([0, 1], [2, 3])]
        products = [(g,) + bank for g in range(GROUPS) for bank in (wide if g < LAST else narrow)]

        gpsimd_pieces = [0, 1, 2, 4]
        w1_halves = [(g, half) for g in range(1, GROUPS) for half in range(2)]

        due, tiles, tiles_next = [], [], []
        for step in range(CHUNKS):
            first_stage(step)
            if step % PACK == 0 and step > 0:
                quantize_z(step // PACK - 1)
            apply_gains(due)
            tiles.extend(tiles_next)
            tiles_next = [
                (g, a)
                for g, t, start, width in due
                if t == PACK - 1
                for a in range(start // P, (start + width) // P)
            ]
            due = []
            if 2 <= step < 2 + PIECES:
                quantize_blend(step - 2)
            if step % 2 == 1:
                pair = step // 2
                if pair < len(w1_halves):
                    quantize_w1(*w1_halves[pair])
                else:
                    quantize_y(gpsimd_pieces[pair - len(w1_halves)])
                if pair + 2 < len(w1_halves):
                    interleave_w1(*w1_halves[pair + 2], True)
                else:
                    round_y(gpsimd_pieces[pair + 2 - len(w1_halves)], True)
                scale_hidden(pair)
            if step == CHUNKS - 2:
                store_codes(0)
                round_y(3, False)
            if 1 <= step < 1 + PIECES:
                for h in range(TIME_PASSES):
                    copy = nc.vector.tensor_copy if step == 1 and h == 1 else nc.scalar.copy
                    blend_turned[step - 1, h] = turn_rows(blend_raw[step - 1], h, copy)
            for place in range(3):
                if (step + place) % 2 == 0:
                    if step >= PACK * products[0][0] + PACK - 1 + STAGE2_LAG:
                        due.extend(second_stage(*products.pop(0)))
                elif tiles:
                    on_vector = step % 2 == 1 and place == 2
                    store_tile(*tiles.pop(0), nc.vector.tensor_copy if on_vector else nc.scalar.copy)

        quantize_z(LAST)
        apply_gains(due)
        last_gains = []
        for tile in tiles:
            store_tile(*tile)
            last_gains.append(second_stage(*products.pop(0)))
        store_codes(1)
        apply_gains(last_gains[0])
        quantize_y(2)
        apply_gains(last_gains[1])
        quantize_y(3)
        apply_gains(last_gains[2])
        store_codes(2)

        for piece in range(PIECES):
            due = second_stage(*products.pop(0)) + second_stage(*products.pop(0))
            n = gpsimd_pieces[-1] + 2 * piece
            round_y(n + 1, False)
            quantize_y(n)
            store_tile(LAST - 1, 2 * piece)
            store_tile(LAST - 1, 2 * piece + 1)
            store_codes(n - 1)
            store_codes(n)
            apply_gains(due)
            round_y(n + 2, False)
            quantize_y(n + 1)

        final = GROUPS * PIECES - 1
        round_y(final, False)
        quantize_y(final - 1)
        quantize_y(final)
        for piece in range(PIECES):
            store_tile(LAST, 2 * piece)
            store_tile(LAST, 2 * piece + 1)
            store_codes(LAST * PIECES + piece)

        scale_words = out_2.bitcast(I32)
        for q in range(P // 32):
            nc.sync.dma_start(
                out=scale_words[:, PACK * q : PACK * q + PACK, :],
                in_=y_scales[32 * q : 32 * q + PACK * GROUPS, :].bitcast(I32),
            )
